import numpy as np, ml_dtypes
CORES = [48,51,52,55]
N = 4
BF = ml_dtypes.bfloat16
def gentries(a):
    return np.ascontiguousarray(a.reshape(8, 16, -1).transpose(0, 2, 1)).reshape(8, -1)
def gtable(e):
    e = np.asarray(e); return np.ascontiguousarray(e.reshape(8, -1, 16).transpose(0, 2, 1)).reshape(128, -1).astype(np.int32)
V, L, A, S, C, RO = 8192, 2048, 512, 256, 4, 3
def ringed(o, s):
    n = np.empty(V, np.int64); f = np.roll(o, -1); f[np.append(s[1:], V) - 1] = o[s]; n[o] = f
    return n
def longrings(rng):
    n = np.empty((N, 8, V), np.int64)
    for q in range(N):
        for g in range(8):
            m = int(rng.integers(1, 7)); s = (1 + rng.permutation(15)[:m - 1]) * (V // 16) + rng.integers(0, V // 32, m - 1)
            n[q, g] = ringed(rng.permutation(V), np.sort(np.concatenate([np.zeros(1, np.int64), s])))
    return n
def parts(rng):
    lev = np.array([64, 128, 256], np.float32)
    x = (rng.random((N, 8, 16, V), dtype=np.float32) * rng.choice(lev, (N, 8, 1, V))).astype(np.int32)
    z = (rng.random((N, 8, 16, L), dtype=np.float32) * rng.choice(lev, (N, 8, 1, L))).astype(np.int32)
    w = rng.integers(0, 256, (N, 8, 16, 1)); w[:, :, 0] |= 1
    return x, z, w
def turns(z, w):
    return 1 + (np.sum(w * z, axis=2) & (C - 1))
def stand(n, u, c):
    back = np.argsort(n, axis=-1)
    for i in range(C): u = np.where(i < c, np.take_along_axis(back, u, 2), u)
    return u
def pack(x, z, w, n, c):
    return {"cards": x.reshape(N, 128, V).astype(np.float32).astype(BF), "z0": z.reshape(N, 128, L).astype(np.float32).astype(BF), "wt": np.ascontiguousarray(w.reshape(N, 128, 1)).astype(np.int32),
            "cur": np.stack([gtable(a) for a in c]), "nx": n.astype(np.int32)}
def setup_inputs(rng):
    x, z, w = parts(rng); size = rng.permutation(np.tile(np.array([V, 2 * A, A // 2, A // 4]), 2 * N)).reshape(N, 8, 1)
    pool = np.argsort(rng.random((N, 8, V)), axis=-1)
    return pack(x, z, w, longrings(rng), np.take_along_axis(pool, (rng.random((N, 8, L)) * size).astype(np.int64), 2))
def setup_inputs_room(rng):
    x, z, w = parts(rng); n = longrings(rng); u = np.empty((N, 8, L), np.int64)
    many = rng.choice(np.array([0, 2, S - 2, S, S + 2, A]), (N, 8)); many[0] = (S, S + 2, A, S - 2, 2, 0, S, S + 2)
    for g, m in enumerate((S, S, S - 2, S + 2, A, A, 0, 2)): many[1 + g % (N - 1), (g + 1) % 8] = m
    w[0, 2] = 0
    for q in range(N):
        for g in range(8):
            p = rng.permutation(V); k = p[:A].reshape(A // 2, 2).copy(); rest = rng.permutation(A // 2)[int(many[q, g]) // 2:]
            if (q, g) == (0, 5):
                k[np.arange(A // 2), rng.integers(0, 2, A // 2)] = p[A]; k[int(rng.integers(0, A // 2))] = p[A]
            else:
                b = int(rng.integers(0, len(rest) // 2 + 1)); k[rest[b:2 * b], 0] = k[rest[:b], 1]; k[rest[2 * b:], 1] = k[rest[2 * b:], 0]
            u[q, g] = np.concatenate([k.reshape(-1), p[rng.integers(0, 2 * A, L - A)]])
    return pack(x, z, w, n, stand(n, u, turns(z, w)))
def setup_inputs_ties(rng):
    x, z, w = parts(rng); i = np.arange(16).reshape(1, 1, 16, 1)
    h = ((5 * i + rng.integers(0, 16, (N, 8, 1, V))) & 15) < rng.integers(7, 11, (N, 8, 1, V))
    x[:, ::2] = np.where(h, 255, 0)[:, ::2]; z[:, ::2] = np.minimum(z[:, ::2], 254)
    base = rng.choice(np.array([0, 100, 253]), (N, 4, 1, 1)); base[0, :, 0, 0] = (0, 100, 253, 0)
    x[:, 1::2] = base + rng.integers(0, 3, (N, 4, 16, V)); z[:, 1::2] = base + rng.integers(0, 2, (N, 4, 16, L))
    w[:, 2] = 0; w[:, 3] = 255; w[:, 4] = C * rng.integers(0, 256 // C, (N, 16, 1)); w[:, 5, 1:] = 0
    w[:, 7] = 0; w[:, 7, 0] = 1; z[:, 7, 0] |= C - 1
    return pack(x, z, w, longrings(rng), rng.integers(0, V, (N, 8, L)))
def setup_inputs_close(rng):
    x, z, w = parts(rng); n = np.empty((N, 8, V), np.int64); u = np.empty((N, 8, L), np.int64)
    w[:, 3::4, 0] = 1; w[:, 3::4, 1:] = C * rng.integers(0, 256 // C, (N, 2, 15, 1)); z[:, 3::4, :8, :A] = 255
    for q in range(N):
        for g in range(8):
            o = rng.permutation(V); a = int(rng.integers(0, V)); k = rng.permutation(A)
            if g % 4 == 0:
                o = np.arange(V); a = 1024 * int(rng.integers(0, V // 1024)) + int(rng.integers(240, 273))
            if g % 4 == 1: k = np.arange(A)
            if g % 4 == 3:
                t = 2 * rng.permutation(A // 2).reshape(2, A // 4); k = np.stack([t[0], t[1], t[0] + 1, t[1] + 1], axis=1).reshape(-1)
                i = o[(a + t[0] + 1) % V]; x[q, g, 0, i] = (x[q, g, 0, i] | (C - 1)) - 1
                i = o[(a + t[1] + 2) % V]; x[q, g, 0, i] = x[q, g, 0, i] | (C - 1)
            n[q, g] = ringed(o, np.zeros(1, np.int64))
            u[q, g] = o[(a + np.concatenate([k, rng.integers(-2 * C, A, L - A)])) % V]
    return pack(x, z, w, n, stand(n, u, turns(z, w)))
def setup_inputs_rings(rng):
    x, z, w = parts(rng); n = np.empty((N, 8, V), np.int64); c = rng.integers(0, V, (N, 8, L))
    for q in range(N):
        for g in range(8):
            m = (1, 2, 3, C, C + 1, 0, V, 7)[(q + g) % 8]; o = np.arange(V) if m == V else rng.permutation(V)
            n[q, g] = ringed(o, np.arange(0, V, m) if m > 0 else np.unique(np.concatenate([np.zeros(1, np.int64), rng.integers(0, V, V // 8)])))
    c[:, :, :8] = rng.choice(np.array([0, V - 1]), (N, 8, 8)); c[:, :, A - 2] = 0; c[:, :, A - 1] = V - 1; c[:, :, A] = 0; c[:, :, L - 1] = V - 1
    return pack(x, z, w, n, c)
def setup_inputs_spread(rng):
    x, z, w = parts(rng)
    def uneven(k):
        a = np.minimum((np.exp2(8 * rng.random((N, 8, 1, k))) * rng.random((N, 8, 16, k), dtype=np.float32)).astype(np.int32), 255); e = rng.random((N, 8, 1, k))
        return np.where(e < 0.04, 0, np.where(e > 0.96, 255, a))
    x = uneven(V); z = uneven(L); w = np.minimum(np.exp2(8 * rng.random((N, 8, 16, 1))).astype(np.int64), 255)
    return pack(x, z, w, longrings(rng), (V * rng.random((N, 8, L)) ** 3).astype(np.int64))
def check_inputs(d):
    bad = []
    for k in ("cards", "z0"):
        a = d[k].astype(np.float32)
        if not (np.min(a) >= 0 and np.max(a) <= 255 and np.all(np.floor(a) == a)): bad.append("whole numbers of " + k)
    for k, hi in (("wt", 255), ("cur", V - 1)):
        if np.min(d[k]) < 0 or np.max(d[k]) > hi: bad.append("range of " + k)
    if not np.all(np.sort(d["nx"], axis=-1) == np.arange(V)): bad.append("each row of nx holds every card once")
    return bad
def reference(cards, z0, wt, cur, nx):
    x = cards.astype(np.float32).astype(np.int32).reshape(N, 8, 16, V); z = z0.astype(np.float32).astype(np.int32).reshape(N, 8, 16, L)
    w = wt.astype(np.int32).reshape(N, 8, 16, 1); nxt = nx.astype(np.int64); v = np.stack([gentries(a) for a in cur]).astype(np.int64)
    for rnd in range(RO):
        c = 1 + (np.sum(w * z, axis=2) & (C - 1))
        for s in range(C):
            go = s < c
            v = np.where(go, np.take_along_axis(nxt, v, 2), v)
            cd = np.take_along_axis(x, v[:, :, None, :], 3)
            up = go & (np.add.reduce((cd > z).astype(np.int32), axis=2) >= 9)
            z = np.where(up[:, :, None, :], (z + cd) >> 1, z)
        u = v; v = np.take_along_axis(nxt, u, 2)
        z = np.abs(z - np.take_along_axis(x, v[:, :, None, :], 3))
        a = u[:, :, :A]; b = v[:, :, :A]
        key = np.arange(N * 8).reshape(N, 8, 1) * V + a
        cnt = np.bincount(key.reshape(-1), minlength=N * 8 * V).reshape(N, 8, V)
        alone = (np.take_along_axis(cnt, a, 2) == 1).reshape(N, 8, A // 2, 2)
        cut = np.repeat(np.all(alone, axis=3), 2, axis=2)
        i, g, j = np.nonzero(cut)
        nxt[i, g, a[i, g, j]] = b[i, g, j ^ 1]
        if rnd < RO - 1:
            top = [[b[q, h][cut[q, h]][:S] for h in range(8)] for q in range(N)]
            sent = [[x[q, h][:, top[q][h]] for h in range(8)] for q in range(N)]
            for q in range(N):
                for h in range(8):
                    r = (q + 1 + (h + rnd) % (N - 1)) % N; k = (h + 1) % 8; m = min(len(top[q][h]), len(top[r][k]))
                    x[r, k][:, top[r][k][:m]] = sent[q][h][:, :m]
    return {"yz": z.reshape(N, 128, L).astype(np.float32).astype(BF), "yc": v.astype(np.float32), "yn": nxt.astype(np.float32)}

@@ -1,0 +1,570 @@
+import numpy as np
+from concourse.bass import DstId, RemoteDMATransfer
+from concourse.mybir import dt, AluOpType, AxisListType, ActivationFunctionType
+
+V, L, A, S, RO = 8192, 2048, 512, 256, 3
+H = L // 2
+HW = H // 16
+M = 8388608.0
+K = 32768.0
+SW = 264
+NDMA = 60
+
+SCRATCH = {}
+for _t, _l in (("float32", dict(W=V + S, Z=L, hA=H + 8, hB=H + 8, tm=128, prod=512, uf=32, upk=32, tc=32, Sc=32, ae=32, arr=S,
+                                nmin=4, q1=16, q2=16, q3=16, wf=4, one32=128, I32=128, nI32=128, Pp=128, pf=4, J0=64, J=64,
+                                JK=64, S0=128, S1=128, Dc=32, Ec=32, Dk=16)),
+               ("bfloat16", dict(NT=V + A, CT=V, db=L, cmpb=L, zbf=L, cv=L, Nw=L, N5=L, EQ=512, hT=64, OH=32 * 192,
+                                 Hs=512, aw=A, nb=32, CV=S, snd0=SW, snd1=SW, land0=3 * SW, land1=3 * SW, hb=512, lb=512,
+                                 one16=144, BigN=144, BigV=144, BigW=144, BigC=144, BigP=144, SelT=16, ioA=64, ioB=128,
+                                 I16=128, KI=128, Blk=128, U0=128, U1=128, Sh2=128, BigM=144, pk2=S, Psh=384)),
+               ("int32", dict(ci=128, cj=128, nxi=512, nxl=512, curi=128, wi=4, wj=4, pi=4, pj=4)),
+               ("uint16", dict(XI=1280, UI=128, I2=128, CI=32, PI=16, TI=16, DI=16))):
+    for _n, _c in _l.items():
+        SCRATCH[_n] = ("sbuf", [128, _c], _t)
+for _b in range(8):
+    SCRATCH["ps%d" % _b] = ("psum", [128, 512], "float32")
+SEMAPHORES = ["sv", "sa", "sp", "sg", "arr0", "arr1", "sent"] + ["d%d" % _i for _i in range(NDMA)]
+
+COST = {"cyc": 0.00104, "pe": 0.0007, "G": 1.56, "SC": 3.8, "sync": 0.12, "fix": 0.04, "dma0": 2.0, "rate": 250000.0}
+VARY = [{"G": 1.04, "SC": 1.6}, {"G": 2.08, "SC": 6.0}, {"sync": 0.3, "fix": 0.08}]
+OPT = {"addm": "va", "wsplit": "aavvvvvv", "z0": "aaaa", "rev": "pppppv", "sign": "aaaaaaaa", "fill": 2560, "pre": 2,
+       "seed": 0, "iters": 3000, "look": 0.1, "temp": 0.4}
+ALU = AluOpType
+ACT = ActivationFunctionType
+PLAN = {}
+
+
+def build(g, core, T, topo, C, O):
+    rank = T.rank_of(core)
+    N = len(T.cores)
+    ops = []
+    cyc = C["cyc"]
+    ID = ACT.Identity
+
+    def op(eng, fn, r, w, dur, bank=None, kind="c", ext=None, nbytes=0):
+        ops.append({"eng": eng, "fn": fn, "r": list(r), "w": list(w), "dur": dur, "bank": bank, "kind": kind,
+                    "ext": ext, "nb": nbytes})
+
+    def dv(n):
+        return max(64, n) * cyc + C["fix"] * 0.5
+
+    def vts(out, in0, s1, s2, o0, o1, r, w, n, bank=None):
+        if o1 is None:
+            op("v", lambda: g.vector.tensor_scalar(out, in0, s1, None, o0), r, w, dv(n), bank)
+        else:
+            op("v", lambda: g.vector.tensor_scalar(out, in0, s1, s2, o0, o1), r, w, dv(n), bank)
+
+    def vtt(out, in0, in1, o, r, w, n, bank=None):
+        op("v", lambda: g.vector.tensor_tensor(out, in0, in1, o), r, w, dv(n), bank)
+
+    def vcp(out, in_, r, w, n, bank=None):
+        op("v", lambda: g.vector.tensor_copy(out, in_), r, w, dv(n), bank)
+
+    def vset(out, w, n):
+        op("v", lambda: g.vector.memset(out, 0.0), [], w, dv(n))
+
+    def act(out, in_, f, r, w, n, bias=0.0, scale=1.0, bank=None):
+        op("a", lambda: g.scalar.activation(out, in_, f, bias=bias, scale=scale), r, w, max(64, n) * cyc + C["fix"], bank)
+
+    def mm(lst, r, w, bank):
+        def fn():
+            ins = None
+            for k, (o, l, x) in enumerate(lst):
+                ins = g.tensor.matmul(o, l, x, k == 0, k == len(lst) - 1)
+            return ins
+        cy = sum(max(64, x.shape[1]) * (4 if str(x.dtype).find("32") >= 0 else 1) for (o, l, x) in lst)
+        op("p", fn, r, w, cy * C["pe"] + C["fix"], bank)
+
+    def dma(q, out, in_, r, w, nbytes, **kw):
+        e = {"s": g.sync, "a": g.scalar, "g": g}[q]
+        op(q, lambda: e.dma_start(out, in_, **kw), r, w, 0.1 if q != "g" else 1.0, None, "dma", None, nbytes)
+
+    def gio(name, pat, base, cm, out=None):
+        o = T[name][:] if out is None else out
+        kw = {} if name == "pi" else {"allow_small_or_imprecise_dtypes": True}
+        op("g", lambda: g.iota(o, pat, base, cm, **kw), [], [name], 0.13 + 2 * o.shape[1] * cyc)
+
+    def gsel(name, src, pat, cmp, base, cm, out=None):
+        o = T[name][:] if out is None else out
+        op("g", lambda: g.affine_select(o, T[src][:, 0:o.shape[1]], pat, cmp, 0.0, base, cm), [src], [name],
+           0.17 + 2 * o.shape[1] * cyc)
+
+    ps = [T["ps%d" % b] for b in range(8)]
+    W = T.W
+    Wc = W[:, 0:V]
+    hh = [T.hA, T.hB]
+    NCC = 8
+    CW = V // NCC
+    WK = ["Wc%d" % k for k in range(NCC)]
+    ZK = [["Z%d_%d" % (h, k) for k in range(2)] for h in range(2)]
+    DK = [["db%d_%d" % (h, k) for k in range(2)] for h in range(2)]
+    FK = [["zf%d_%d" % (h, k) for k in range(2)] for h in range(2)]
+    CTK = ["CT%d" % k for k in range(NCC)]
+    NK = ["NTh", "NTl"]
+    GE, EQL = ALU.is_ge, ALU.is_equal
+
+    def xi(r, s, h):
+        o = ((r % 2) * 5 + s) * 128 + h * HW
+        return T.XI[:, o:o + HW], "xi%d_%d_%d" % (r % 2, s, h), o
+
+    dma("s", T.nxi[:], T.nx[:], [], ["nxi"], 128 * 2048)
+    dma("a", T.curi[:], T.cur[:], [], ["curi"], 128 * 512)
+    dma("a", T.wi[:, 0:1], T.wt[:], [], ["wi"], 128 * 64)
+    dma("s", T.zbf[:], T.z0[:], [], FK[0] + FK[1], 128 * 4096)
+    F = O["fill"]
+    vset(T.NT[:, 0:F], ["NT0"], F // 2)
+    vset(T.NT[:, 2 * F:V + A], ["NT2"], (V + A - 2 * F) // 2)
+    act(T.NT[:, F:2 * F], T.NT[:, 0:F], ID, ["NT0"], ["NT1"], F)
+    vset(T.hA[:, H:H + 8], ["hz0"], 8)
+    vset(T.hB[:, H:H + 8], ["hz1"], 8)
+    P = O["pre"]
+    dma("s", T.CT[:, 0:P * CW], T.cards[:, 0:P * CW], [], CTK[0:P], 128 * CW * 2 * P)
+    vts(T.nxl[:], T.nxi[:], 127, None, ALU.bitwise_and, None, ["nxi"], ["nxl"], 512)
+    vtt(T.hb[:], T.nxi[:], T.nxl[:], ALU.subtract, ["nxi", "nxl"], ["hb"], 1024)
+    vcp(T.lb[:], T.nxl[:], ["nxl"], ["lb"], 512)
+    dma("s", T.NT[0:128:16, 0:V], T.hb[:], ["hb"], ["NTh"], 128 * 1024)
+    ops[-1]["after"] = ["NT0", "NT1", "NT2"]
+    dma("s", T.NT[1:128:16, 0:V], T.lb[:], ["lb"], ["NTl"], 128 * 1024)
+    ops[-1]["after"] = ["NT0", "NT1", "NT2"]
+    for k in range(P, NCC):
+        dma("s", T.CT[:, k * CW:(k + 1) * CW], T.cards[:, k * CW:(k + 1) * CW], [], CTK[k:k + 1], 128 * CW * 2)
+    for h in range(2):
+        a, key, o = xi(0, 0, h)
+        vcp(a, T.curi[:, h * HW:(h + 1) * HW], ["curi"], [key], HW)
+
+    gio("one16", [[0, 144]], 1, 0)
+    gsel("BigN", "one16", [[-16, 9], [0, 16]], GE, 0, 1)
+    gsel("BigN", "BigN", [[16, 9], [1000, 16]], GE, 1 - 15000, -1)
+    gio("BigV", [[0, 144]], -int(K), 0)
+    gsel("BigV", "BigV", [[-16, 9], [0, 16]], GE, 0, 1)
+    gsel("BigV", "BigV", [[16, 9], [1000, 16]], GE, 15 - 15000, -1)
+    gio("pi", [[0, 1]], 0, 1, T.pi[:, 0:1])
+    gio("J0", [[16, 64]], 0, 0)
+    gio("one32", [[0, 128]], 1, 0)
+    gsel("I32", "one32", [[-1, 128]], EQL, 0, 1)
+    gio("KI", [[0, 128]], 16 * int(K), 0)
+    gsel("KI", "KI", [[-1, 128]], EQL, 0, 1)
+    gsel("SelT", "one16", [[-16, 8], [-1, 2]], EQL, 0, 1)
+    gio("ioA", [[128, 64]], 0, 0)
+    gio("ioB", [[1, 128]], 0, 0)
+    gsel("Pp", "one32", [[-2, 64], [1, 2]], EQL, -1, 1)
+    gio("BigP", [[0, 144]], int(K), 0)
+    gsel("BigP", "BigP", [[-16, 9], [0, 16]], EQL, 16, 1)
+    gsel("BigP", "BigP", [[0, 9], [-1, 16]], GE, 1, 0)
+    gsel("Blk", "one16", [[-16, 8], [0, 16]], GE, 0, 1)
+    gsel("Blk", "Blk", [[16, 8], [0, 16]], GE, 15, -1)
+    for e in range(2):
+        gsel("U%d" % e, "Blk", [[-16, 8], [-2, 16]], GE, 16 * e, 1)
+        gsel("S%d" % e, "one32", [[-16, 8], [0, 16]], GE, 0, 1)
+        gsel("S%d" % e, "S%d" % e, [[16, 8], [0, 16]], GE, 15, -1)
+        gsel("S%d" % e, "S%d" % e, [[-16, 8], [-2, 16]], EQL, 16 * e, 1)
+    gsel("Sh2", "one16", [[-1, 128]], EQL, 2, 1)
+    gsel("BigM", "one16", [[-16, 9], [0, 16]], GE, -2, 1)
+    gsel("BigM", "BigM", [[16, 9], [1000, 16]], GE, 3 - 15000, -1)
+    gio("nI32", [[0, 128]], -1, 0)
+    gsel("nI32", "nI32", [[-1, 128]], EQL, 0, 1)
+    gsel("I16", "one16", [[-1, 128]], EQL, 0, 1)
+    gio("Psh", [[0, 384]], 0, 0)
+    for gr in range(8):
+        o = (gr % 3) * 128 + ((gr + 1) % 8) * 16
+        gsel("Psh", "one16", [[-1, 16]], EQL, -16 * gr, 1, T.Psh[:, o:o + 16])
+    gio("sndc0", [[0, SW - S]], 0, 0, T.snd0[:, S:SW])
+    gio("sndc1", [[0, SW - S]], 0, 0, T.snd1[:, S:SW])
+
+    vts(T.wj[:, 0:1], T.wi[:, 0:1], 3, None, ALU.bitwise_and, None, ["wi"], ["wj"], 1)
+    vcp(T.wf[:, 0:1], T.wj[:, 0:1], ["wj"], ["wf"], 1)
+    vts(T.BigC[:], T.BigV[:], T.wf[:, 0:1], -1.0 / K, ALU.mult, ALU.mult, ["BigV", "wf"], ["BigC"], 144)
+    vts(T.pj[:, 0:1], T.pi[:, 0:1], 15, None, ALU.bitwise_and, None, ["pi"], ["pj"], 1)
+    vcp(T.pf[:, 0:1], T.pj[:, 0:1], ["pj"], ["pf"], 1)
+    act(T.J[:], T.J0[:], ID, ["J0", "pf"], ["J"], 64, bias=T.pf[:, 0:1])
+    if "v" in O["sign"]:
+        act(T.BigW[:], T.BigV[:], ID, ["BigV"], ["BigW"], 144, scale=2.0)
+    act(T.JK[:], T.J[:], ID, ["J"], ["JK"], 64, bias=-K)
+    act(T.Dc[:], T.J[:, 0:32], ID, ["J"], ["Dc"], 32, bias=V + 2.5 * K)
+    act(T.Ec[:], T.J[:, 0:32], ID, ["J"], ["Ec"], 32, bias=510.0, scale=-1.0)
+    act(T.Dk[:], T.J[:, 0:16], ID, ["J"], ["Dk"], 16, bias=float(V))
+
+    def addc(e, out, in_, c, r, w, n):
+        if e == "a":
+            act(out, in_, ID, r, w, n, bias=c)
+        else:
+            vts(out, in_, c, None, ALU.add, None, r, w, n)
+
+    for h in range(2):
+        for k in range(2):
+            o = h * H + k * 512
+            addc(O["z0"][2 * h + k], T.Z[:, o:o + 512], T.zbf[:, o:o + 512], M, [FK[h][k]], [ZK[h][k]], 512)
+    for k in range(NCC):
+        addc(O["wsplit"][k], W[:, k * CW:(k + 1) * CW], T.CT[:, k * CW:(k + 1) * CW], M, [CTK[k]], [WK[k]], CW)
+
+    def agather(out, oo, win, off, fo, ncol, r, w, bias=0.0, sub=1):
+        st = ncol // sub
+        for k in range(sub):
+            act(out[:, oo + 16 * k * st:oo + 16 * (k + 1) * st], win.indirect(off[:, fo + k * st:fo + (k + 1) * st]),
+                ID, r, [w + "_%d" % k], int(16 * st * C["G"]), bias=bias)
+        return [w + "_%d" % k for k in range(sub)]
+
+    def wrap(out, big, off, src, so, n, r, w, bank, extra=()):
+        mm([(out, big[:, off(i):off(i) + 128], src[:, so + i:so + n:16]) for i in range(16)] + list(extra), r, w, bank)
+
+    offN = lambda i: 15 - i
+    NTw = T.NT[:, 0:V]
+
+    def steps(r, ss):
+        for s in ss:
+            for h in range(2):
+                sl = slice(h * HW, (h + 1) * HW)
+                wd = slice(h * H, (h + 1) * H)
+                a, key, o = xi(r, s, h)
+                if r == 0 and s == 1:
+                    vtt(T.db[:, wd], T.CT[:].indirect(a), T.zbf[:, wd], ALU.subtract, CTK + [key] + FK[h],
+                        DK[h] + ["ctr%d" % h], H * C["G"] + 30)
+                else:
+                    vtt(T.db[:, wd], Wc.indirect(a), T.Z[:, wd], ALU.subtract, WK + [key] + ZK[h], DK[h], H * C["G"] + 30)
+                if O["sign"][2 * (s - 1) + h] == "a":
+                    act(T.cmpb[:, wd], T.db[:, wd], ACT.Sign, DK[h], ["cmp%d" % h], H, bias=-0.5)
+                    big = "BigV"
+                else:
+                    vts(T.cmpb[:, wd], T.db[:, wd], 0.0, -0.5, ALU.is_gt, ALU.add, DK[h], ["cmp%d" % h], H // 2)
+                    big = "BigW"
+                act(hh[h][:, 0:H], T.db[:, wd], ID, DK[h], ["h%d" % h], H, bias=-0.25, scale=0.5)
+                pq = ps[2 + h][:, 0:HW]
+                ex = [(pq, T.KI[:], T.EQ[:, h * 256 + e * HW:h * 256 + (e + 1) * HW]) for e in range(s - 1)]
+                wrap(pq, T[big], offN, T.cmpb, h * H, H, ["cmp%d" % h, big, "KI"] + ["eq%d_%d" % (h, e) for e in range(s - 1)],
+                     ["pq%d" % h], 2 + h, ex)
+                vtt(T.tm[:, sl], pq, T.JK[:], ALU.max, ["pq%d" % h, "JK"], ["tm%d" % h], HW, 2 + h)
+                vts(T.I2[:, sl], T.tm[:, sl], K, float(H), ALU.add, ALU.min, ["tm%d" % h], ["i2%d" % h], HW)
+                vtt(T.Z[:, wd], hh[h][:].indirect(T.I2[:, sl]), T.Z[:, wd], ALU.add,
+                    ["h%d" % h, "hz%d" % h, "i2%d" % h] + ZK[h], ZK[h], H * C["G"] + 30)
+
+    for r in range(RO):
+        last = r == RO - 1
+        for s in range(1, 5):
+            for h in range(2):
+                a, key, o = xi(r, s - 1, h)
+                ks = agather(T.Nw, h * H, NTw, T.XI, o, HW, NK + [key], "Nw%d" % h)
+                px = ps[h][:, (s - 1) * HW:s * HW]
+                wrap(px, T.BigN, offN, T.Nw, h * H, H, ks + ["BigN"], ["px%d_%d" % (h, s)], h)
+                a, key, o = xi(r, s, h)
+                vcp(a, px, ["px%d_%d" % (h, s)], [key], HW, h)
+        n5 = []
+        cvk = []
+        for h in range(2):
+            sl = slice(h * HW, (h + 1) * HW)
+            pc = ps[2 + h][:, 128:192]
+            wrap(pc, T.BigC, offN, T.zbf, h * H, H, FK[h] + ["BigC"], ["pc%d" % h], 2 + h)
+            vcp(T.ci[:, sl], pc, ["pc%d" % h], ["ci%d" % h], HW, 2 + h)
+            vts(T.cj[:, sl], T.ci[:, sl], 3, None, ALU.bitwise_and, None, ["ci%d" % h], ["cj%d" % h], HW)
+            for s in range(4):
+                o = h * 256 + s * HW
+                vts(T.EQ[:, o:o + HW], T.cj[:, sl], float(s), None, EQL, None, ["cj%d" % h], ["eq%d_%d" % (h, s)], HW)
+            vtt(T.prod[:, h * 256:(h + 1) * 256], ps[h][:, 0:256], T.EQ[:, h * 256:(h + 1) * 256], ALU.mult,
+                ["px%d_%d" % (h, s) for s in range(1, 5)] + ["eq%d_%d" % (h, s) for s in range(4)], ["prod%d" % h], 256, h)
+            pu = ps[h][:, 256:320]
+            mm([(pu, T.I32[:], T.prod[:, h * 256 + s * HW:h * 256 + (s + 1) * HW]) for s in range(4)],
+               ["I32", "prod%d" % h], ["pu%d" % h], h)
+            vcp(T.UI[:, sl], pu, ["pu%d" % h], ["ui%d" % h], HW, h)
+            if h == 0:
+                act(T.uf[:], ps[0][:, 256:288], ID, ["pu0"], ["uf"], 32, bank=0)
+            ks = agather(T.N5, h * H, NTw, T.UI, h * HW, HW, NK + ["ui%d" % h], "N5%d" % h, sub=2)
+            n5.append(ks)
+            pv = ps[h][:, 320:384]
+            wrap(pv, T.BigN, offN, T.N5, h * H, H, ks + ["BigN"], ["pv%d" % h], h)
+            a, key, o = xi(r + 1, 0, h)
+            vcp(a, pv, ["pv%d" % h], [key], HW, h)
+            if O["rev"][2 * r + h] != "v":
+                cvk.append(agather(T.cv, h * H, Wc, T.XI, o, HW, WK + [key], "cv%d" % h, bias=-M, sub=2))
+            else:
+                cvk.append(None)
+        nA = n5[0][0]
+        vkey, vo = xi(r + 1, 0, 0)[1:]
+        if last:
+            dma("g", T.yc[:], T.N5[0:128:16, :], n5[0] + n5[1], ["yc"], 8 * 8192)
+            dma("g", T.yc[:], T.N5[1:128:16, :], n5[0] + n5[1] + ["yc"], ["yc"], 8 * 8192, accum_op=ALU.add)
+        steps(r, [1])
+        for t in range(4):
+            mm([(ps[7][:, 16 * t:16 * t + 16], T.N5[:, 128 * t:128 * (t + 1)], T.SelT[:])], [nA, "SelT"], ["pT%d" % t], 7)
+        act(T.hT[:], ps[7][:, 0:64], ID, ["pT%d" % t for t in range(4)], ["hT"], 64, bank=7)
+        mm([(ps[7][:, 64:96], T.Pp[:], T.uf[:])], ["Pp", "uf"], ["pP"], 7)
+        act(T.upk[:], ps[7][:, 64:96], ID, ["pP"], ["upk"], 32, bias=2.5 * K, bank=7)
+        for gr in range(8):
+            lst = []
+            kk = []
+            for t in range(4):
+                o = (gr * 4 + t) * 192
+                c = 16 * t + 2 * gr
+                vts(T.OH[:, o:o + 64], T.ioA[:], T.hT[:, c:c + 1], None, EQL, None, ["ioA", "hT"], ["oa%d" % o], 32)
+                vts(T.OH[:, o + 64:o + 192], T.ioB[:], T.hT[:, c + 1:c + 2], None, EQL, None, ["ioB", "hT"], ["ob%d" % o], 64)
+                kk += ["oa%d" % o, "ob%d" % o]
+                lst.append((ps[6][64 * (gr % 2):64 * (gr % 2) + 64, 128 * (gr // 2):128 * (gr // 2) + 128],
+                            T.OH[:, o:o + 64], T.OH[:, o + 64:o + 192]))
+            mm(lst, kk, ["pH%d" % gr], 6)
+        act(T.Hs[:], ps[6][:], ID, ["pH%d" % gr for gr in range(8)], ["Hs"], 512, bank=6)
+        for q in range(4):
+            dma("s", T.CT[32 * q:32 * q + 32:16, :], T.Hs[:, 128 * q:128 * (q + 1)], ["Hs"], ["CH%d" % q], 128 * 256)
+            if r == 0:
+                ops[-1]["after"] = WK + ["ctr0", "ctr1"]
+        agather(T.aw, 0, T.CT[:], T.XI, vo, 32, CTK + ["CH%d" % q for q in range(4)] + [vkey], "aw")
+        pa = ps[7][:, 96:128]
+        wrap(pa, T.BigP, lambda i: 16 - (i & ~1), T.aw, 0, A, ["aw_0", "BigP"], ["pa"], 7)
+        vtt(ps[7][:, 128:160], pa, T.upk[:], ALU.max, ["pa", "upk"], ["pt"], 32, 7)
+        if not last:
+            vts(T.nb[:], pa, 2.5 * K, 0.5, ALU.is_gt, ALU.mult, ["pa"], ["nb"], 32, 7)
+        vtt(T.tc[:], ps[7][:, 128:160], T.Dc[:], ALU.min, ["pt", "Dc"], ["tc"], 32, 7)
+        vts(T.CI[:], T.tc[:], -2.5 * K, None, ALU.add, None, ["tc"], ["CI"], 32)
+        vcp(T.NT[:].indirect(T.CI[:]), T.N5[:, 0:A], ["CI", nA], NK, A * C["SC"] + 30)
+        if last:
+            dma("g", T.yn[:], T.NT[0:128:16, 0:V], ["NTh"], ["yn"], 8 * 32768)
+            dma("g", T.yn[:], T.NT[1:128:16, 0:V], ["NTl", "yn"], ["yn"], 8 * 32768 * 2, accum_op=ALU.add, max_dma_last_dim=4096)
+        if not last:
+            snd = T["snd%d" % r]
+            land = T["land%d" % r]
+            pS, pR, pk = ps[7][:, 160:176], ps[7][:, 192:208], ps[7][:, 224:240]
+            mm([(pS, T.Blk[:], T.nb[:, e:32:2]) for e in range(2)], ["Blk", "nb"], ["pS"], 7)
+            op("v", lambda: g.vector.tensor_tensor_scan(T.Sc[:, 0:16], T.one32[:, 0:16], ps[7][:, 160:176], 0.0, ALU.mult, ALU.add),
+               ["pS", "one32"], ["Sc"], dv(32), 7)
+            vtt(T.ae[:], T.nb[:], T.Ec[:], ALU.mult, ["nb", "Ec"], ["ae"], 64)
+            mm([(pR, T["U%d" % e][:], T.nb[:, e:32:2]) for e in range(2)] + [(pR, T["S%d" % e][:], T.ae[:, e:32:2]) for e in range(2)]
+               + [(pR, T.I32[:], T.J[:, 0:16]), (pR, T.nI32[:], T.Sc[:, 0:16])],
+               ["U0", "U1", "S0", "S1", "nb", "I32", "J", "ae", "nI32", "Sc"], ["pR"], 7)
+            vcp(T.PI[:], pR, ["pR"], ["PI"], 16, 7)
+            mm([(ps[7][:, 256:512], T.I16[:], T.N5[:, 0:A:2]), (ps[7][:, 256:512], T.Sh2[:], T.N5[:, 1:A:2])],
+               ["I16", "Sh2", nA], ["pp"], 7)
+            act(T.pk2[:], ps[7][:, 256:512], ID, ["pp"], ["pk2"], S, bank=7)
+            vcp(T.CV[:].indirect(T.PI[:]), T.pk2[:], ["PI", "pk2"], ["CV"], S * C["SC"] + 30)
+            mm([(pk, T["BigM" if i % 2 else "BigN"][:, 15 - i:143 - i], T.CV[:, i // 2:128:8]) for i in range(16)],
+               ["CV", "BigN", "BigM"], ["pk"], 7)
+            vcp(T.TI[:], pk, ["pk"], ["TI"], 16, 7)
+            agather(snd, 0, Wc, T.TI, 0, 16, WK + ["TI"], "snd%d" % r, bias=-M)
+            act(snd[:, S:S + 1], T.Sc[:, 15:16], ID, ["Sc"], ["sndc%d" % r], 1, bias=float(A), scale=-2.0)
+
+            def send(snd=snd, land=land, r=r):
+                tr = []
+                for d in range(N - 1):
+                    dst = T.cores[(rank + 1 + d) % N]
+                    rid, pid, se = topo.addr(dst)
+                    en = topo.engines(core, dst)[4 * d:4 * d + 4]
+                    tr.append(RemoteDMATransfer(dst_ids=[DstId(rid=rid, pnc=pid)], dma_engine_mask=sum(1 << e for e in en),
+                                                remote_sem=T.sem["arr%d" % r], src=snd[:], dst=land[:, d * SW:(d + 1) * SW]))
+                g.remote_dma_fused(tr, local_sem=T.sem.sent)
+                return None
+            op("g", send, ["snd%d_0" % r, "sndc%d" % r], ["land%d" % r], 1.0, None, "rem", ("arr%d" % r, 12), 128 * 528 * 3)
+        steps(r, [2, 3, 4])
+        for h in range(2):
+            if cvk[h] is None:
+                a, key, o = xi(r + 1, 0, h)
+                for k in range(2):
+                    wd = slice(h * H + k * 512, h * H + (k + 1) * 512)
+                    vtt(T.db[:, wd], Wc.indirect(T.XI[:, o + 32 * k:o + 32 * k + 32]), T.Z[:, wd], ALU.subtract,
+                        WK + [key, ZK[h][k]], [DK[h][k]], 512 * C["G"] + 30)
+        if not last:
+            pd = ps[6][:, 0:SW]
+            mm([(pd, T.Psh[:, ((d - r) % 3) * 128:((d - r) % 3) * 128 + 128], land[:, d * SW:(d + 1) * SW]) for d in range(3)],
+               ["Psh", "land%d" % r], ["pd"], 6)
+            act(T.arr[:], ps[6][:, 0:S], ID, ["pd"], ["arr"], S, bias=M, bank=6)
+            vtt(T.nmin[:, 0:1], ps[6][:, S:S + 1], snd[:, S:S + 1], ALU.min, ["pd", "sndc%d" % r], ["nmin"], 1, 6)
+            vts(T.q1[:], T.J[:, 0:16], T.nmin[:, 0:1], K, GE, ALU.mult, ["J", "nmin"], ["q1"], 16)
+            vtt(T.q2[:], pk, T.q1[:], ALU.max, ["pk", "q1"], ["q2"], 16, 7)
+            vtt(T.q3[:], T.q2[:], T.Dk[:], ALU.min, ["q2", "Dk"], ["q3"], 32)
+            vcp(T.DI[:], T.q3[:], ["q3"], ["DI"], 16)
+            vcp(W[:].indirect(T.DI[:]), T.arr[:], ["DI", "arr"], WK, S * C["SC"] + 30)
+        for h in range(2):
+            for k in range(2):
+                o = h * H + k * 512
+                b = 4 + k
+                if cvk[h] is None:
+                    act(T.zbf[:, o:o + 512], T.db[:, o:o + 512], ACT.Abs, [DK[h][k]], [FK[h][k]], 512)
+                else:
+                    mm([(ps[b][:], T.I16[:], T.cv[:, o:o + 512]), (ps[b][:], T.nI32[:], T.Z[:, o:o + 512])],
+                       ["I16", "nI32", cvk[h][k], ZK[h][k]], ["pz%d" % b], b)
+                    act(T.zbf[:, o:o + 512], ps[b][:], ACT.Abs, ["pz%d" % b], [FK[h][k]], 512, bias=M, bank=b)
+                if last:
+                    dma("s", T.yz[:, o:o + 512], T.zbf[:, o:o + 512], [FK[h][k]], ["yz%d" % o], 128 * 1024)
+                else:
+                    addc(O["addm"][k], T.Z[:, o:o + 512], T.zbf[:, o:o + 512], M, [FK[h][k]], [ZK[h][k]], 512)
+    return ops
+
+
+def depend(ops):
+    lastw, readers, bankl, prevq = {}, {}, {}, {}
+    for i, o in enumerate(ops):
+        d = set()
+        for k in o["r"] + o.get("after", []):
+            if k in lastw:
+                d.add(lastw[k])
+        for k in o["w"]:
+            if k in lastw:
+                d.add(lastw[k])
+            d.update(readers.get(k, []))
+        b = o["bank"]
+        if b is not None:
+            run = bankl.get(b)
+            if run is None or run[0] != o["eng"]:
+                run = [o["eng"], [], run[1] if run else []]
+                bankl[b] = run
+            d.update(run[2])
+            run[1].append(i)
+        d.discard(i)
+        o["dep"] = sorted(d)
+        o["prev"] = prevq.get(o["eng"]) if o["eng"] in "sg" else None
+        prevq[o["eng"]] = i
+        for k in o["r"]:
+            readers.setdefault(k, []).append(i)
+        for k in o["w"]:
+            lastw[k] = i
+            readers[k] = []
+    return ops
+
+
+def listsched(ops, C, succ, left0, pr, look):
+    n = len(ops)
+    left = list(left0)
+    free = {e: 0.0 for e in "vapgs"}
+    ready = {e: [] for e in "vapgs"}
+    fin, start, rt = [0.0] * n, [0.0] * n, [0.0] * n
+    pipe, sy, d0, rate = 0.0, C["sync"], C["dma0"], C["rate"]
+    cand, seq = {}, []
+    for i in range(n):
+        if left[i] == 0:
+            ready[ops[i]["eng"]].append(i)
+    for _ in range(n):
+        best = None
+        for e in "vapgs":
+            if e not in cand:
+                c = ready[e]
+                if not c:
+                    continue
+                t0 = max(free[e], min(rt[i] for i in c)) + look
+                i = max((i for i in c if rt[i] <= t0), key=lambda i: pr[i])
+                cand[e] = (max(free[e], rt[i]), i)
+            if best is None or cand[e][0] < best[0]:
+                best = cand[e]
+        t, i = best
+        o = ops[i]
+        e = o["eng"]
+        ready[e].remove(i)
+        seq.append(i)
+        start[i] = t
+        free[e] = fin[i] = t + o["dur"]
+        del cand[e]
+        if o["kind"] != "c":
+            pipe = max(pipe, free[e] + d0 * 0.7) + o["nb"] / rate
+            fin[i] = pipe + d0 * 0.3
+        for j, real in succ[i]:
+            if real and fin[i] + sy > rt[j]:
+                rt[j] = fin[i] + sy
+            left[j] -= 1
+            if left[j] == 0:
+                ready[ops[j]["eng"]].append(j)
+                cand.pop(ops[j]["eng"], None)
+    return seq, start, max(fin)
+
+
+def replay(ops, C, seq):
+    free = {e: 0.0 for e in "vapgs"}
+    fin = [0.0] * len(ops)
+    pipe, sy, d0, rate = 0.0, C["sync"], C["dma0"], C["rate"]
+    for i in seq:
+        o = ops[i]
+        t = free[o["eng"]]
+        for j in o["dep"]:
+            if fin[j] + sy > t:
+                t = fin[j] + sy
+        free[o["eng"]] = fin[i] = t + o["dur"]
+        if o["kind"] != "c":
+            pipe = max(pipe, fin[i] + d0 * 0.7) + o["nb"] / rate
+            fin[i] = pipe + d0 * 0.3
+    return max(fin)
+
+
+def plan(mk, C, O, vary):
+    ops = mk(C)
+    alt = [(mk(dict(C, **m)), dict(C, **m)) for m in vary]
+    n = len(ops)
+    succ, left = [[] for _ in range(n)], [0] * n
+    for i, o in enumerate(ops):
+        for j in sorted(set(o["dep"] + ([o["prev"]] if o["prev"] is not None else []))):
+            succ[j].append((i, j in o["dep"]))
+            left[i] += 1
+    pr = np.zeros(n)
+    for i in range(n - 1, -1, -1):
+        o = ops[i]
+        pr[i] = o["dur"] + (0.0 if o["kind"] == "c" else C["dma0"] + o["nb"] / C["rate"]) \
+            + max([pr[j] + C["sync"] for j, _ in succ[i]] + [0.0])
+
+    def score(p):
+        seq, start, end = listsched(ops, C, succ, left, p.tolist(), O["look"])
+        return np.array([end] + [replay(o2, C2, seq) for o2, C2 in alt]), seq, np.array(start)
+    rs = np.random.RandomState(O["seed"])
+    a0, seq, st = score(pr)
+    w = np.array([2.0] + [1.0] * len(alt)) / a0
+    w = w / np.dot(a0, w) * a0[0]
+    cur = best = float(np.dot(a0, w))
+    out = (seq, a0, st)
+    for it in range(O["iters"]):
+        p = pr.copy()
+        k = rs.randint(4)
+        if k == 0:
+            a = rs.randint(n)
+            p[a:a + rs.randint(1, 40)] += rs.normal(0, 4.0)
+        elif k == 2:
+            p[rs.randint(n, size=3)] += rs.normal(0, 3.0, 3)
+        else:
+            t = rs.rand() * st.max()
+            m = (abs(st - t) < 3) & (rs.rand(n) < 0.3) if k == 1 else abs(st - t) < 6
+            p[m] += rs.normal(0, 2.0 if k == 1 else 0.5, m.sum())
+        a, seq, start = score(p)
+        s = float(np.dot(a, w))
+        if s <= cur + O["temp"] * (1 - it / O["iters"]) * rs.rand():
+            cur, pr, st = s, p, start
+            if s < best:
+                best, out = s, (seq, a, start)
+    return out
+
+
+def rank_program(g, core, T, topo):
+    if T.rank_of(core) is None:
+        return
+    mk = lambda C: depend(build(g, core, T, topo, C, OPT))
+    if "seq" not in PLAN:
+        PLAN["seq"] = plan(mk, COST, OPT, VARY)[0]
+    ops = mk(COST)
+    order = {e: [i for i in PLAN["seq"] if ops[i]["eng"] == e] for e in "vapgs"}
+    queue = {"v": g.vector, "a": g.scalar, "p": g.tensor, "g": g, "s": g.sync}
+    final = {}
+    nd = 0
+    for e in "vapgs":
+        cnt = 0
+        for i in order[e]:
+            o = ops[i]
+            if o["kind"] == "c":
+                cnt += 1
+                o["sig"] = ("s" + e, cnt)
+            elif o["kind"] == "dma":
+                o["sig"] = ("d%d" % nd, 16)
+                nd += 1
+            else:
+                o["sig"] = o["ext"]
+                final["sent"] = final.get("sent", 0) + 12
+            final[o["sig"][0]] = o["sig"][1]
+    for e in "vapgs":
+        seen = {}
+        q = queue[e]
+        for i in order[e]:
+            o = ops[i]
+            need = {}
+            for j in o["dep"]:
+                s, v = ops[j]["sig"]
+                need[s] = max(need.get(s, 0), v)
+            for s in sorted(need):
+                if need[s] > seen.get(s, 0):
+                    q.wait_ge(T.sem[s], need[s])
+                    seen[s] = need[s]
+            ins = o["fn"]()
+            if o["kind"] != "rem":
+                ins.then_inc(T.sem[o["sig"][0]], 1 if o["kind"] == "c" else 16)
+        if e == "g":
+            for s in sorted(final):
+                if final[s] > seen.get(s, 0):
+                    q.wait_ge(T.sem[s], final[s])

@@ -5,19 +5,23 @@ from concourse.mybir import dt, AluOpType, AxisListType, ActivationFunctionType
 V, L, A, S, RO = 8192, 2048, 512, 256, 3
 H = L // 2
 HW = H // 16
-M = 8388608.0
+B = 512
+E = 1024.0
 K = 32768.0
+XO = 16384.0
 SW = 264
-NDMA = 60
+NDMA = 100
 
 SCRATCH = {}
-for _t, _l in (("float32", dict(W=V + S, Z=L, hA=H + 8, hB=H + 8, tm=128, prod=512, uf=32, upk=32, tc=32, Sc=32, ae=32, arr=S,
+for _t, _l in (("float32", dict(WZ=L + V + S, Zi=L, Y=V + A, v32=A, xf=256, tm=128, prod=512, uf=32, upk=32, tc=32, Sc=32, ae=32, arr=S,
                                 nmin=4, q1=16, q2=16, q3=16, wf=4, one32=128, I32=128, nI32=128, Pp=128, pf=4, J0=64, J=64,
-                                JK=64, S0=128, S1=128, Dc=32, Ec=32, Dk=16)),
-               ("bfloat16", dict(NT=V + A, CT=V, db=L, cmpb=L, zbf=L, cv=L, Nw=L, N5=L, EQ=512, hT=64, OH=32 * 192,
+                                JE=128, JA=128, S0=128, S1=128, Dc=32, Ec=32, Dk=16)),
+               ("float16", dict(Z16=L)),
+               ("bfloat16", dict(NT=V + A, CT=V, Nc=L, cmpb=L, zbf=L, cv=L, Nw=L, N5=L, EQ=512, hT=64, OH=32 * 192,
                                  Hs=512, aw=A, nb=32, CV=S, snd0=SW, snd1=SW, land0=3 * SW, land1=3 * SW, hb=512, lb=512,
-                                 one16=144, BigN=144, BigV=144, BigW=144, BigC=144, BigP=144, SelT=16, ioA=64, ioB=128,
-                                 I16=128, KI=128, Blk=128, U0=128, U1=128, Sh2=128, BigM=144, pk2=S, Psh=384)),
+                                 one16=144, BigN=144, BigV=144, BigC=144, BigP=144, SelT=16, ioA=64, ioB=128,
+                                 I16=128, nI16=128, Ih=128, Blk=128, U0=128, U1=128, Sh2=128, BigM=144, pk2=S, Psh=384,
+                                 BigK=144, KI=128)),
                ("int32", dict(ci=128, cj=128, nxi=512, nxl=512, curi=128, wi=4, wj=4, pi=4, pj=4)),
                ("uint16", dict(XI=1280, UI=128, I2=128, CI=32, PI=16, TI=16, DI=16))):
     for _n, _c in _l.items():
@@ -26,10 +30,12 @@ for _b in range(8):
     SCRATCH["ps%d" % _b] = ("psum", [128, 512], "float32")
 SEMAPHORES = ["sv", "sa", "sp", "sg", "arr0", "arr1", "sent"] + ["d%d" % _i for _i in range(NDMA)]
 
-COST = {"cyc": 0.00104, "pe": 0.0007, "G": 1.56, "SC": 3.8, "sync": 0.12, "fix": 0.04, "dma0": 2.0, "rate": 250000.0}
-VARY = [{"G": 1.04, "SC": 1.6}, {"G": 2.08, "SC": 6.0}, {"sync": 0.3, "fix": 0.08}]
-OPT = {"addm": "va", "wsplit": "aavvvvvv", "z0": "aaaa", "rev": "pppppv", "sign": "aaaaaaaa", "fill": 2560, "pre": 2,
-       "seed": 0, "iters": 3000, "look": 0.1, "temp": 0.4}
+COST = {"cyc": 0.00084, "pe": 0.0005, "G": 1.5, "SC": 3.6, "sync": 0.11, "fix": 0.005, "dma0": 2.0, "rate": 380000.0}
+VARY = [{"G": 1.1, "SC": 2.0}, {"G": 1.9, "SC": 5.0, "cyc": 0.0011}, {"sync": 0.22, "fix": 0.03}, {"pe": 0.00083}]
+OPT = {"how": [["eeee", "eeae"], ["eaee", "eeae"], ["eaee", "eeae"]], "chain": ["vavaaaaa", "aaaaaaaa", "aaaaaaaa"], "twin": ["g" * 16] * 3, "conv": "aaavavav",
+       "sub": (1, 1), "f16": True, "csub": 1, "fill": 2560, "pre": 2,
+       "pace": (13, 7.8, 1, 112), "skew": 0.5, "hop": 0.8, "hops": "vava", "spare": 0.6, "eager": 200.0, "seed": 0, "iters": 3000, "temp": 0.15,
+       "moves": 1500, "heat": 0.1, "far": 0.6}
 ALU = AluOpType
 ACT = ActivationFunctionType
 PLAN = {}
@@ -46,8 +52,11 @@ def build(g, core, T, topo, C, O):
         ops.append({"eng": eng, "fn": fn, "r": list(r), "w": list(w), "dur": dur, "bank": bank, "kind": kind,
                     "ext": ext, "nb": nbytes})
 
+    def after(keys):
+        ops[-1]["after"] = list(keys)
+
     def dv(n):
-        return max(64, n) * cyc + C["fix"] * 0.5
+        return max(64, n) * cyc + C["fix"]
 
     def vts(out, in0, s1, s2, o0, o1, r, w, n, bank=None):
         if o1 is None:
@@ -61,19 +70,26 @@ def build(g, core, T, topo, C, O):
     def vcp(out, in_, r, w, n, bank=None):
         op("v", lambda: g.vector.tensor_copy(out, in_), r, w, dv(n), bank)
 
-    def vset(out, w, n):
-        op("v", lambda: g.vector.memset(out, 0.0), [], w, dv(n))
+    def vset(out, w, n, c=0.0):
+        op("v", lambda: g.vector.memset(out, c), [], w, dv(n))
 
     def act(out, in_, f, r, w, n, bias=0.0, scale=1.0, bank=None):
-        op("a", lambda: g.scalar.activation(out, in_, f, bias=bias, scale=scale), r, w, max(64, n) * cyc + C["fix"], bank)
+        op("a", lambda: g.scalar.activation(out, in_, f, bias=bias, scale=scale), r, w, dv(n), bank)
 
-    def mm(lst, r, w, bank):
+    def addc(e, out, in_, c, r, w, n, bank=None):
+        if e == "a":
+            act(out, in_, ID, r, w, n, bias=c, bank=bank)
+        else:
+            vts(out, in_, c, None, ALU.add, None, r, w, n, bank)
+
+    def mm(lst, r, w, bank, how="group"):
         def fn():
             ins = None
             for k, (o, l, x) in enumerate(lst):
-                ins = g.tensor.matmul(o, l, x, k == 0, k == len(lst) - 1)
+                ins = g.tensor.matmul(o, l, x, how == "each" or (how in ("group", "open") and k == 0),
+                                      how == "each" or (how in ("group", "close") and k == len(lst) - 1))
             return ins
-        cy = sum(max(64, x.shape[1]) * (4 if str(x.dtype).find("32") >= 0 else 1) for (o, l, x) in lst)
+        cy = sum(max(min(64, l.shape[1]), x.shape[1]) * (4 if str(x.dtype).find("32") >= 0 else 1) for (o, l, x) in lst)
         op("p", fn, r, w, cy * C["pe"] + C["fix"], bank)
 
     def dma(q, out, in_, r, w, nbytes, **kw):
@@ -91,66 +107,67 @@ def build(g, core, T, topo, C, O):
            0.17 + 2 * o.shape[1] * cyc)
 
     ps = [T["ps%d" % b] for b in range(8)]
-    W = T.W
-    Wc = W[:, 0:V]
-    hh = [T.hA, T.hB]
+    WZ = T.WZ
+    Wc = WZ[:, H:H + V]
     NCC = 8
     CW = V // NCC
-    WK = ["Wc%d" % k for k in range(NCC)]
-    ZK = [["Z%d_%d" % (h, k) for k in range(2)] for h in range(2)]
-    DK = [["db%d_%d" % (h, k) for k in range(2)] for h in range(2)]
-    FK = [["zf%d_%d" % (h, k) for k in range(2)] for h in range(2)]
-    CTK = ["CT%d" % k for k in range(NCC)]
-    NK = ["NTh", "NTl"]
+    WK = ["W%d" % k for k in range(NCC)]
+    NK = ["NTh", "NTl"] + ["NTc%d" % q for q in range(4)]
     GE, EQL = ALU.is_ge, ALU.is_equal
+    PX, PC = 0, 256
 
     def xi(r, s, h):
         o = ((r % 2) * 5 + s) * 128 + h * HW
         return T.XI[:, o:o + HW], "xi%d_%d_%d" % (r % 2, s, h), o
 
+    def zat(k):
+        o = (k // 2) * (H + V + S) + (k % 2) * B
+        return WZ[:, o:o + B]
+
     dma("s", T.nxi[:], T.nx[:], [], ["nxi"], 128 * 2048)
     dma("a", T.curi[:], T.cur[:], [], ["curi"], 128 * 512)
     dma("a", T.wi[:, 0:1], T.wt[:], [], ["wi"], 128 * 64)
-    dma("s", T.zbf[:], T.z0[:], [], FK[0] + FK[1], 128 * 4096)
+    dma("s", T.zbf[:], T.z0[:], [], ["zf%d" % k for k in range(4)], 128 * 4096)
     F = O["fill"]
     vset(T.NT[:, 0:F], ["NT0"], F // 2)
     vset(T.NT[:, 2 * F:V + A], ["NT2"], (V + A - 2 * F) // 2)
     act(T.NT[:, F:2 * F], T.NT[:, 0:F], ID, ["NT0"], ["NT1"], F)
-    vset(T.hA[:, H:H + 8], ["hz0"], 8)
-    vset(T.hB[:, H:H + 8], ["hz1"], 8)
-    P = O["pre"]
-    dma("s", T.CT[:, 0:P * CW], T.cards[:, 0:P * CW], [], CTK[0:P], 128 * CW * 2 * P)
+    vset(WZ[:, H + V:H + V + S], ["dump"], S)
+
+    def load(k):
+        dma("s", T.CT[:, k * CW:(k + 1) * CW], T.cards[:, k * CW:(k + 1) * CW], [], ["CT%d" % k], 128 * CW * 2)
+        addc(O["conv"][k], WZ[:, H + k * CW:H + (k + 1) * CW], T.CT[:, k * CW:(k + 1) * CW], E - 0.5, ["CT%d" % k], [WK[k]], CW)
+
+    for k in range(O["pre"]):
+        load(k)
     vts(T.nxl[:], T.nxi[:], 127, None, ALU.bitwise_and, None, ["nxi"], ["nxl"], 512)
     vtt(T.hb[:], T.nxi[:], T.nxl[:], ALU.subtract, ["nxi", "nxl"], ["hb"], 1024)
     vcp(T.lb[:], T.nxl[:], ["nxl"], ["lb"], 512)
     dma("s", T.NT[0:128:16, 0:V], T.hb[:], ["hb"], ["NTh"], 128 * 1024)
-    ops[-1]["after"] = ["NT0", "NT1", "NT2"]
+    after(["NT0", "NT1", "NT2"])
     dma("s", T.NT[1:128:16, 0:V], T.lb[:], ["lb"], ["NTl"], 128 * 1024)
-    ops[-1]["after"] = ["NT0", "NT1", "NT2"]
-    for k in range(P, NCC):
-        dma("s", T.CT[:, k * CW:(k + 1) * CW], T.cards[:, k * CW:(k + 1) * CW], [], CTK[k:k + 1], 128 * CW * 2)
+    after(["NT0", "NT1", "NT2"])
+    for k in range(O["pre"], NCC):
+        load(k)
     for h in range(2):
         a, key, o = xi(0, 0, h)
         vcp(a, T.curi[:, h * HW:(h + 1) * HW], ["curi"], [key], HW)
 
     gio("one16", [[0, 144]], 1, 0)
-    gsel("BigN", "one16", [[-16, 9], [0, 16]], GE, 0, 1)
-    gsel("BigN", "BigN", [[16, 9], [1000, 16]], GE, 1 - 15000, -1)
-    gio("BigV", [[0, 144]], -int(K), 0)
-    gsel("BigV", "BigV", [[-16, 9], [0, 16]], GE, 0, 1)
+    gsel("BigV", "one16", [[-16, 9], [0, 16]], GE, 0, 1)
+    gsel("BigN", "BigV", [[16, 9], [1000, 16]], GE, 1 - 15000, -1)
     gsel("BigV", "BigV", [[16, 9], [1000, 16]], GE, 15 - 15000, -1)
+    gsel("I16", "one16", [[-1, 128]], EQL, 0, 1)
     gio("pi", [[0, 1]], 0, 1, T.pi[:, 0:1])
     gio("J0", [[16, 64]], 0, 0)
     gio("one32", [[0, 128]], 1, 0)
     gsel("I32", "one32", [[-1, 128]], EQL, 0, 1)
-    gio("KI", [[0, 128]], 16 * int(K), 0)
-    gsel("KI", "KI", [[-1, 128]], EQL, 0, 1)
     gsel("SelT", "one16", [[-16, 8], [-1, 2]], EQL, 0, 1)
     gio("ioA", [[128, 64]], 0, 0)
     gio("ioB", [[1, 128]], 0, 0)
     gsel("Pp", "one32", [[-2, 64], [1, 2]], EQL, -1, 1)
     gio("BigP", [[0, 144]], int(K), 0)
-    gsel("BigP", "BigP", [[-16, 9], [0, 16]], EQL, 16, 1)
+    gsel("BigP", "BigP", [[-16, 9], [0, 16]], EQL, 12, 1)
     gsel("BigP", "BigP", [[0, 9], [-1, 16]], GE, 1, 0)
     gsel("Blk", "one16", [[-16, 8], [0, 16]], GE, 0, 1)
     gsel("Blk", "Blk", [[16, 8], [0, 16]], GE, 15, -1)
@@ -162,9 +179,6 @@ def build(g, core, T, topo, C, O):
     gsel("Sh2", "one16", [[-1, 128]], EQL, 2, 1)
     gsel("BigM", "one16", [[-16, 9], [0, 16]], GE, -2, 1)
     gsel("BigM", "BigM", [[16, 9], [1000, 16]], GE, 3 - 15000, -1)
-    gio("nI32", [[0, 128]], -1, 0)
-    gsel("nI32", "nI32", [[-1, 128]], EQL, 0, 1)
-    gsel("I16", "one16", [[-1, 128]], EQL, 0, 1)
     gio("Psh", [[0, 384]], 0, 0)
     for gr in range(8):
         o = (gr % 3) * 128 + ((gr + 1) % 8) * 16
@@ -174,120 +188,160 @@ def build(g, core, T, topo, C, O):
 
     vts(T.wj[:, 0:1], T.wi[:, 0:1], 3, None, ALU.bitwise_and, None, ["wi"], ["wj"], 1)
     vcp(T.wf[:, 0:1], T.wj[:, 0:1], ["wj"], ["wf"], 1)
-    vts(T.BigC[:], T.BigV[:], T.wf[:, 0:1], -1.0 / K, ALU.mult, ALU.mult, ["BigV", "wf"], ["BigC"], 144)
+    vts(T.BigC[:], T.BigV[:], T.wf[:, 0:1], None, ALU.mult, None, ["BigV", "wf"], ["BigC"], 72)
     vts(T.pj[:, 0:1], T.pi[:, 0:1], 15, None, ALU.bitwise_and, None, ["pi"], ["pj"], 1)
     vcp(T.pf[:, 0:1], T.pj[:, 0:1], ["pj"], ["pf"], 1)
+    for name, src, n, scale in (("nI16", "I16", 128, -1.0), ("Ih", "I16", 128, 0.5), ("KI", "I16", 128, 16 * K),
+                                ("nI32", "I32", 128, -1.0), ("BigK", "BigV", 144, -K)):
+        act(T[name][:], T[src][:], ID, [src], [name], n, scale=scale)
     act(T.J[:], T.J0[:], ID, ["J0", "pf"], ["J"], 64, bias=T.pf[:, 0:1])
-    if "v" in O["sign"]:
-        act(T.BigW[:], T.BigV[:], ID, ["BigV"], ["BigW"], 144, scale=2.0)
-    act(T.JK[:], T.J[:], ID, ["J"], ["JK"], 64, bias=-K)
+    for name, lo in (("JE", 9 * K), ("JA", K)):
+        if name == "JE" or "a" in str(O["how"]):
+            act(T[name][:, 0:HW], T.J[:], ID, ["J"], [name + "0"], HW, bias=XO - lo, scale=-1.0)
+            act(T[name][:, HW:2 * HW], T.J[:], ID, ["J"], [name + "1"], HW, bias=XO - lo + V + S)
     act(T.Dc[:], T.J[:, 0:32], ID, ["J"], ["Dc"], 32, bias=V + 2.5 * K)
     act(T.Ec[:], T.J[:, 0:32], ID, ["J"], ["Ec"], 32, bias=510.0, scale=-1.0)
     act(T.Dk[:], T.J[:, 0:16], ID, ["J"], ["Dk"], 16, bias=float(V))
 
-    def addc(e, out, in_, c, r, w, n):
-        if e == "a":
-            act(out, in_, ID, r, w, n, bias=c)
-        else:
-            vts(out, in_, c, None, ALU.add, None, r, w, n)
-
-    for h in range(2):
-        for k in range(2):
-            o = h * H + k * 512
-            addc(O["z0"][2 * h + k], T.Z[:, o:o + 512], T.zbf[:, o:o + 512], M, [FK[h][k]], [ZK[h][k]], 512)
-    for k in range(NCC):
-        addc(O["wsplit"][k], W[:, k * CW:(k + 1) * CW], T.CT[:, k * CW:(k + 1) * CW], M, [CTK[k]], [WK[k]], CW)
-
-    def agather(out, oo, win, off, fo, ncol, r, w, bias=0.0, sub=1):
+    def agather(out, oo, win, off, fo, ncol, r, w, sub=1, eng="a", bias=0.0):
         st = ncol // sub
         for k in range(sub):
-            act(out[:, oo + 16 * k * st:oo + 16 * (k + 1) * st], win.indirect(off[:, fo + k * st:fo + (k + 1) * st]),
-                ID, r, [w + "_%d" % k], int(16 * st * C["G"]), bias=bias)
+            o = out[:, oo + 16 * k * st:oo + 16 * (k + 1) * st]
+            i = win.indirect(off[:, fo + k * st:fo + (k + 1) * st])
+            addc(eng[k % len(eng)], o, i, bias, r, [w + "_%d" % k], 16 * st * C["G"] + 65)
         return [w + "_%d" % k for k in range(sub)]
 
-    def wrap(out, big, off, src, so, n, r, w, bank, extra=()):
-        mm([(out, big[:, off(i):off(i) + 128], src[:, so + i:so + n:16]) for i in range(16)] + list(extra), r, w, bank)
+    def wrap(out, big, off, src, so, n, r, w, bank):
+        mm([(out, big[:, off(i):off(i) + 128], src[:, so + i:so + n:16]) for i in range(16)], r, w, bank)
 
     offN = lambda i: 15 - i
     NTw = T.NT[:, 0:V]
 
-    def steps(r, ss):
+    def twice(r, s, k, src, key, scale, bias, bank):
+        zi = T.Zi[:, k * B:(k + 1) * B]
+        act(zi, src, ID, [key], ["zi%d" % k], B, bias=bias, scale=scale, bank=bank)
+        e = O["twin"][r][4 * s + k]
+        if e == "a":
+            act(zat(k), src, ID, [key], ["zw%d" % k], B, bias=bias, scale=scale, bank=bank)
+        elif e == "g":
+            op("g", lambda: g.affine_select(zat(k), zi, [[0, B]], GE, 0.0, 0, 0), ["zi%d" % k], ["zw%d" % k], 0.17 + 2 * B * cyc)
+        else:
+            dma("s", zat(k), zi, ["zi%d" % k], ["zw%d" % k], 128 * 2048)
+
+    def step(r, s, h, cvk):
+        a, key, o = xi(r, s, h)
+        sl = slice(h * HW, (h + 1) * HW)
+        ch = (2 * h, 2 * h + 1)
+        zo = h * (H + V + S)
+        zk = ["zw%d" % k for k in ch]
+        how = O["how"][r][h][s - 1]
+        st = H // O["sub"][0] if how == "e" else B
+        for c in range(0, H, st):
+            if how == "e":
+                ks = [k for k in ch if c <= (k % 2) * B < c + st]
+                vtt(T.cmpb[:, h * H + c:h * H + c + st], Wc.indirect(T.XI[:, o + c // 16:o + (c + st) // 16]),
+                    T.Zi[:, h * H + c:h * H + c + st], ALU.is_gt, WK + [key] + ["zi%d" % k for k in ks], ["cmp%d" % k for k in ks],
+                    st * C["G"] + 55)
+                ops[-1]["due"] = (r, s, ks[0])
+            else:
+                k = 2 * h + c // B
+                wd, zb = slice(k * B, (k + 1) * B), k % 2
+                ks = agather(T.Nc, k * B, Wc, T.XI, o + c // 16, 32, WK + [key], "nc%d" % k, bias=0.5 - E)
+                mm([(ps[zb][:], T.nI16[:], T.Nc[:, wd])], ["nI16"] + ks, ["b%d" % zb], zb, "open")
+                z = (T.I16, T.zbf, "zf%d" % k, 0.0) if s == 1 else (T.Ih, T.Z16, "z%d" % k, E)
+                mm([(ps[zb][:], z[0][:], z[1][:, wd])], ["I16", "Ih", z[2]], ["b%d" % zb], zb, "close")
+                ops[-1]["due"] = (r, s, k)
+                act(T.cmpb[:, wd], ps[zb][:], ACT.Sign, ["b%d" % zb], ["cmp%d" % k], B, bias=z[3] - 0.5, scale=-1.0, bank=zb)
+        b = 2 + h
+        pq, pt = ps[b][:, 0:HW], ps[b][:, HW:2 * HW]
+        lo, jk = (9 * K, "JE") if how == "e" else (K, "JA")
+        mm([(pq, T.BigK[:, 15 - i:143 - i], T.cmpb[:, h * H + i:(h + 1) * H:16]) for i in range(16)]
+           + [(pq, T.KI[:], T.EQ[:, h * 256 + e * HW:h * 256 + (e + 1) * HW]) for e in range(s - 1)],
+           ["cmp%d" % k for k in ch] + ["BigK", "KI"] + ["eq%d_%d" % (h, e) for e in range(s - 1)], ["b%d" % b], b)
+        sg = 1.0 if h else -1.0
+        xf = T.xf[:, (s % 2) * 128 + h * HW:(s % 2) * 128 + (h + 1) * HW]
+        xk = "xf%d_%d" % (s % 2, h)
+        act(xf, ps[6 + h][:, PX + (s - 1) * HW:PX + s * HW], ID, ["px%d_%d" % (h, s)], [xk], HW, scale=sg,
+            bias=XO - lo - (0 if h else H), bank=6 + h)
+        vtt(pt, pq, xf, ALU.max, ["b%d" % b, xk], ["t%d" % b], HW, b)
+        vtt(T.tm[:, sl], pt, T[jk][:, sl], ALU.min, ["t%d" % b, jk + str(h)], ["tm%d" % h], HW, b)
+        vts(T.I2[:, sl], T.tm[:, sl], lo - XO, sg, ALU.add, ALU.mult, ["tm%d" % h], ["i2%d" % h], HW)
+        win = WZ[:, H:2 * H + V + S] if h else WZ[:, 0:H + V]
+        st = H // O["sub"][1]
+        for c in range(0, H, st):
+            ks = [k for k in ch if c <= (k % 2) * B < c + st]
+            vtt(T.Z16[:, h * H + c:h * H + c + st], win.indirect(T.I2[:, h * HW + c // 16:h * HW + (c + st) // 16]),
+                T.Zi[:, h * H + c:h * H + c + st], ALU.add, WK + zk + ["zi%d" % k for k in ks] + ["i2%d" % h, "dump"],
+                ["z%d" % k for k in ks], st * C["G"] + 55)
+        for k in ch:
+            wd, zb = slice(k * B, (k + 1) * B), k % 2
+            if s < 4 and O["f16"]:
+                twice(r, s, k, T.Z16[:, wd], "z%d" % k, 0.5, 0.0, None)
+            elif s < 4:
+                mm([(ps[zb][:], T.Ih[:], T.Z16[:, wd])], ["Ih", "z%d" % k], ["b%d" % zb], zb)
+                twice(r, s, k, ps[zb][:], "b%d" % zb, 1.0, 0.0, zb)
+            else:
+                mm([(ps[zb][:], T.nI16[:], T.cv[:, wd])], ["nI16", cvk[k]], ["b%d" % zb], zb, "open")
+                mm([(ps[zb][:], T.Ih[:], T.Z16[:, wd])], ["Ih", "z%d" % k], ["b%d" % zb], zb, "close")
+                act(T.zbf[:, wd], ps[zb][:], ACT.Abs, ["b%d" % zb], ["zf%d" % k], B, bias=-E, bank=zb)
+                if r == RO - 1:
+                    dma("s", T.yz[:, wd], T.zbf[:, wd], ["zf%d" % k], ["yz%d" % k], 128 * 1024)
+
+    def steps(r, ss, cvk):
         for s in ss:
             for h in range(2):
-                sl = slice(h * HW, (h + 1) * HW)
-                wd = slice(h * H, (h + 1) * H)
-                a, key, o = xi(r, s, h)
-                if r == 0 and s == 1:
-                    vtt(T.db[:, wd], T.CT[:].indirect(a), T.zbf[:, wd], ALU.subtract, CTK + [key] + FK[h],
-                        DK[h] + ["ctr%d" % h], H * C["G"] + 30)
-                else:
-                    vtt(T.db[:, wd], Wc.indirect(a), T.Z[:, wd], ALU.subtract, WK + [key] + ZK[h], DK[h], H * C["G"] + 30)
-                if O["sign"][2 * (s - 1) + h] == "a":
-                    act(T.cmpb[:, wd], T.db[:, wd], ACT.Sign, DK[h], ["cmp%d" % h], H, bias=-0.5)
-                    big = "BigV"
-                else:
-                    vts(T.cmpb[:, wd], T.db[:, wd], 0.0, -0.5, ALU.is_gt, ALU.add, DK[h], ["cmp%d" % h], H // 2)
-                    big = "BigW"
-                act(hh[h][:, 0:H], T.db[:, wd], ID, DK[h], ["h%d" % h], H, bias=-0.25, scale=0.5)
-                pq = ps[2 + h][:, 0:HW]
-                ex = [(pq, T.KI[:], T.EQ[:, h * 256 + e * HW:h * 256 + (e + 1) * HW]) for e in range(s - 1)]
-                wrap(pq, T[big], offN, T.cmpb, h * H, H, ["cmp%d" % h, big, "KI"] + ["eq%d_%d" % (h, e) for e in range(s - 1)],
-                     ["pq%d" % h], 2 + h, ex)
-                vtt(T.tm[:, sl], pq, T.JK[:], ALU.max, ["pq%d" % h, "JK"], ["tm%d" % h], HW, 2 + h)
-                vts(T.I2[:, sl], T.tm[:, sl], K, float(H), ALU.add, ALU.min, ["tm%d" % h], ["i2%d" % h], HW)
-                vtt(T.Z[:, wd], hh[h][:].indirect(T.I2[:, sl]), T.Z[:, wd], ALU.add,
-                    ["h%d" % h, "hz%d" % h, "i2%d" % h] + ZK[h], ZK[h], H * C["G"] + 30)
+                step(r, s, h, cvk)
 
     for r in range(RO):
         last = r == RO - 1
+        for k in range(4):
+            twice(r, 0, k, T.zbf[:, k * B:(k + 1) * B], "zf%d" % k, 1.0, E, None)
         for s in range(1, 5):
             for h in range(2):
                 a, key, o = xi(r, s - 1, h)
-                ks = agather(T.Nw, h * H, NTw, T.XI, o, HW, NK + [key], "Nw%d" % h)
-                px = ps[h][:, (s - 1) * HW:s * HW]
-                wrap(px, T.BigN, offN, T.Nw, h * H, H, ks + ["BigN"], ["px%d_%d" % (h, s)], h)
+                ks = agather(T.Nw, h * H, NTw, T.XI, o, HW, NK + [key], "Nw%d" % h, O["csub"], O["chain"][r][2 * (s - 1) + h])
+                px = ps[6 + h][:, PX + (s - 1) * HW:PX + s * HW]
+                wrap(px, T.BigN, offN, T.Nw, h * H, H, ks + ["BigN"], ["px%d_%d" % (h, s)], 6 + h)
                 a, key, o = xi(r, s, h)
-                vcp(a, px, ["px%d_%d" % (h, s)], [key], HW, h)
+                vcp(a, px, ["px%d_%d" % (h, s)], [key], HW, 6 + h)
         n5 = []
         cvk = []
         for h in range(2):
+            b = 6 + h
             sl = slice(h * HW, (h + 1) * HW)
-            pc = ps[2 + h][:, 128:192]
-            wrap(pc, T.BigC, offN, T.zbf, h * H, H, FK[h] + ["BigC"], ["pc%d" % h], 2 + h)
-            vcp(T.ci[:, sl], pc, ["pc%d" % h], ["ci%d" % h], HW, 2 + h)
+            pc, pu, pv = (ps[b][:, PC + k * HW:PC + (k + 1) * HW] for k in range(3))
+            wrap(pc, T.BigC, offN, T.zbf, h * H, H, ["zf%d" % (2 * h), "zf%d" % (2 * h + 1), "BigC"], ["pc%d" % h], b)
+            vcp(T.ci[:, sl], pc, ["pc%d" % h], ["ci%d" % h], HW, b)
             vts(T.cj[:, sl], T.ci[:, sl], 3, None, ALU.bitwise_and, None, ["ci%d" % h], ["cj%d" % h], HW)
             for s in range(4):
                 o = h * 256 + s * HW
                 vts(T.EQ[:, o:o + HW], T.cj[:, sl], float(s), None, EQL, None, ["cj%d" % h], ["eq%d_%d" % (h, s)], HW)
-            vtt(T.prod[:, h * 256:(h + 1) * 256], ps[h][:, 0:256], T.EQ[:, h * 256:(h + 1) * 256], ALU.mult,
-                ["px%d_%d" % (h, s) for s in range(1, 5)] + ["eq%d_%d" % (h, s) for s in range(4)], ["prod%d" % h], 256, h)
-            pu = ps[h][:, 256:320]
+            vtt(T.prod[:, h * 256:(h + 1) * 256], ps[b][:, PX:PX + 256], T.EQ[:, h * 256:(h + 1) * 256], ALU.mult,
+                ["px%d_%d" % (h, s) for s in range(1, 5)] + ["eq%d_%d" % (h, s) for s in range(4)], ["prod%d" % h], 256, b)
             mm([(pu, T.I32[:], T.prod[:, h * 256 + s * HW:h * 256 + (s + 1) * HW]) for s in range(4)],
-               ["I32", "prod%d" % h], ["pu%d" % h], h)
-            vcp(T.UI[:, sl], pu, ["pu%d" % h], ["ui%d" % h], HW, h)
+               ["I32", "prod%d" % h], ["pu%d" % h], b)
+            vcp(T.UI[:, sl], pu, ["pu%d" % h], ["ui%d" % h], HW, b)
             if h == 0:
-                act(T.uf[:], ps[0][:, 256:288], ID, ["pu0"], ["uf"], 32, bank=0)
-            ks = agather(T.N5, h * H, NTw, T.UI, h * HW, HW, NK + ["ui%d" % h], "N5%d" % h, sub=2)
+                act(T.uf[:], ps[b][:, PC + HW:PC + HW + 32], ID, ["pu0"], ["uf"], 32, bank=b)
+            ks = agather(T.N5, h * H, NTw, T.UI, h * HW, HW, NK + ["ui%d" % h], "N5%d" % h, 2, "a" if h else O["hops"][1] + "a")
             n5.append(ks)
-            pv = ps[h][:, 320:384]
-            wrap(pv, T.BigN, offN, T.N5, h * H, H, ks + ["BigN"], ["pv%d" % h], h)
+            wrap(pv, T.BigN, offN, T.N5, h * H, H, ks + ["BigN"], ["pv%d" % h], b)
             a, key, o = xi(r + 1, 0, h)
-            vcp(a, pv, ["pv%d" % h], [key], HW, h)
-            if O["rev"][2 * r + h] != "v":
-                cvk.append(agather(T.cv, h * H, Wc, T.XI, o, HW, WK + [key], "cv%d" % h, bias=-M, sub=2))
-            else:
-                cvk.append(None)
+            vcp(a, pv, ["pv%d" % h], [key], HW, b)
+            cvk += agather(T.cv, h * H, Wc, T.XI, o, HW, WK + [key], "cv%d" % h, sub=2, bias=0.5 - E)
         nA = n5[0][0]
         vkey, vo = xi(r + 1, 0, 0)[1:]
         if last:
             dma("g", T.yc[:], T.N5[0:128:16, :], n5[0] + n5[1], ["yc"], 8 * 8192)
             dma("g", T.yc[:], T.N5[1:128:16, :], n5[0] + n5[1] + ["yc"], ["yc"], 8 * 8192, accum_op=ALU.add)
-        steps(r, [1])
-        for t in range(4):
-            mm([(ps[7][:, 16 * t:16 * t + 16], T.N5[:, 128 * t:128 * (t + 1)], T.SelT[:])], [nA, "SelT"], ["pT%d" % t], 7)
-        act(T.hT[:], ps[7][:, 0:64], ID, ["pT%d" % t for t in range(4)], ["hT"], 64, bank=7)
-        mm([(ps[7][:, 64:96], T.Pp[:], T.uf[:])], ["Pp", "uf"], ["pP"], 7)
-        act(T.upk[:], ps[7][:, 64:96], ID, ["pP"], ["upk"], 32, bias=2.5 * K, bank=7)
+        steps(r, [1], cvk)
+        pT, pP, pa, pt, pS, pR, pk = (ps[4][:, a:b] for a, b in ((0, 64), (64, 96), (96, 128), (128, 160), (160, 176),
+                                                                 (192, 208), (224, 240)))
+        mm([(ps[4][:, 16 * t:16 * t + 16], T.N5[:, 128 * t:128 * (t + 1)], T.SelT[:]) for t in range(4)],
+           [nA, "SelT"], ["pT"], 4, "each")
+        addc(O["hops"][0], T.hT[:], pT, 0.0, ["pT"], ["hT"], 64, 4)
+        mm([(pP, T.Pp[:], T.uf[:])], ["Pp", "uf"], ["pP"], 4)
+        act(T.upk[:], pP, ID, ["pP"], ["upk"], 32, bias=2.5 * K, bank=4)
         for gr in range(8):
             lst = []
             kk = []
@@ -296,47 +350,51 @@ def build(g, core, T, topo, C, O):
                 c = 16 * t + 2 * gr
                 vts(T.OH[:, o:o + 64], T.ioA[:], T.hT[:, c:c + 1], None, EQL, None, ["ioA", "hT"], ["oa%d" % o], 32)
                 vts(T.OH[:, o + 64:o + 192], T.ioB[:], T.hT[:, c + 1:c + 2], None, EQL, None, ["ioB", "hT"], ["ob%d" % o], 64)
+                ops[-1]["spare"] = ops[-2]["spare"] = (7 - gr) * O["spare"]
                 kk += ["oa%d" % o, "ob%d" % o]
-                lst.append((ps[6][64 * (gr % 2):64 * (gr % 2) + 64, 128 * (gr // 2):128 * (gr // 2) + 128],
+                lst.append((ps[5][64 * (gr % 2):64 * (gr % 2) + 64, 128 * (gr // 2):128 * (gr // 2) + 128],
                             T.OH[:, o:o + 64], T.OH[:, o + 64:o + 192]))
-            mm(lst, kk, ["pH%d" % gr], 6)
-        act(T.Hs[:], ps[6][:], ID, ["pH%d" % gr for gr in range(8)], ["Hs"], 512, bank=6)
+            mm(lst, kk, ["pH%d" % gr], 5)
+            after(["b5"])
+        act(T.Hs[:], ps[5][:], ID, ["pH%d" % gr for gr in range(8)] + ["b5"], ["Hs"], 512, bank=5)
         for q in range(4):
-            dma("s", T.CT[32 * q:32 * q + 32:16, :], T.Hs[:, 128 * q:128 * (q + 1)], ["Hs"], ["CH%d" % q], 128 * 256)
-            if r == 0:
-                ops[-1]["after"] = WK + ["ctr0", "ctr1"]
-        agather(T.aw, 0, T.CT[:], T.XI, vo, 32, CTK + ["CH%d" % q for q in range(4)] + [vkey], "aw")
-        pa = ps[7][:, 96:128]
-        wrap(pa, T.BigP, lambda i: 16 - (i & ~1), T.aw, 0, A, ["aw_0", "BigP"], ["pa"], 7)
-        vtt(ps[7][:, 128:160], pa, T.upk[:], ALU.max, ["pa", "upk"], ["pt"], 32, 7)
+            dma("s", T.NT[32 * q + 4:32 * q + 32:16, 0:V], T.Hs[:, 128 * q:128 * (q + 1)], ["Hs"], ["NTc%d" % q], 128 * 256)
+        agather(T.aw, 0, NTw, T.XI, vo, 32, NK + [vkey], "aw")
+        wrap(pa, T.BigP, lambda i: 16 - (i & ~1), T.aw, 0, A, ["aw_0", "BigP"], ["pa"], 4)
+        vtt(pt, pa, T.upk[:], ALU.max, ["pa", "upk"], ["pt"], 32, 4)
         if not last:
-            vts(T.nb[:], pa, 2.5 * K, 0.5, ALU.is_gt, ALU.mult, ["pa"], ["nb"], 32, 7)
-        vtt(T.tc[:], ps[7][:, 128:160], T.Dc[:], ALU.min, ["pt", "Dc"], ["tc"], 32, 7)
+            vts(T.nb[:], pa, 2.5 * K, 0.5, ALU.is_gt, ALU.mult, ["pa"], ["nb"], 32, 4)
+        vtt(T.tc[:], pt, T.Dc[:], ALU.min, ["pt", "Dc"], ["tc"], 32, 4)
         vts(T.CI[:], T.tc[:], -2.5 * K, None, ALU.add, None, ["tc"], ["CI"], 32)
-        vcp(T.NT[:].indirect(T.CI[:]), T.N5[:, 0:A], ["CI", nA], NK, A * C["SC"] + 30)
         if last:
-            dma("g", T.yn[:], T.NT[0:128:16, 0:V], ["NTh"], ["yn"], 8 * 32768)
-            dma("g", T.yn[:], T.NT[1:128:16, 0:V], ["NTl", "yn"], ["yn"], 8 * 32768 * 2, accum_op=ALU.add, max_dma_last_dim=4096)
+            dma("g", T.Y[0:128:16, 0:V], T.NT[0:128:16, 0:V], ["NTh"], ["Y"], 8 * 32768)
+            dma("g", T.Y[0:128:16, 0:V], T.NT[1:128:16, 0:V], ["NTl", "Y"], ["Y"], 8 * 32768 * 2, accum_op=ALU.add,
+                max_dma_last_dim=4096)
+            mm([(ps[5][:], T.BigN[:, 15:143], T.N5[:, 0:A])], ["BigN", nA], ["b5"], 5)
+            act(T.v32[:], ps[5][:], ID, ["b5"], ["v32"], A, bank=5)
+            vcp(T.Y[:].indirect(T.CI[:]), T.v32[:], ["CI", "v32", "Y"], ["Y"], A * C["SC"] + 55)
+            dma("s", T.yn[:], T.Y[0:128:16, 0:V], ["Y"], ["yn"], 8 * 32768)
+        else:
+            vcp(T.NT[:].indirect(T.CI[:]), T.N5[:, 0:A], ["CI", nA], NK, A * C["SC"] + 55)
         if not last:
             snd = T["snd%d" % r]
             land = T["land%d" % r]
-            pS, pR, pk = ps[7][:, 160:176], ps[7][:, 192:208], ps[7][:, 224:240]
-            mm([(pS, T.Blk[:], T.nb[:, e:32:2]) for e in range(2)], ["Blk", "nb"], ["pS"], 7)
-            op("v", lambda: g.vector.tensor_tensor_scan(T.Sc[:, 0:16], T.one32[:, 0:16], ps[7][:, 160:176], 0.0, ALU.mult, ALU.add),
-               ["pS", "one32"], ["Sc"], dv(32), 7)
+            mm([(pS, T.Blk[:], T.nb[:, e:32:2]) for e in range(2)], ["Blk", "nb"], ["pS"], 4)
+            op("v", lambda pS=pS: g.vector.tensor_tensor_scan(T.Sc[:, 0:16], T.one32[:, 0:16], pS, 0.0, ALU.mult, ALU.add),
+               ["pS", "one32"], ["Sc"], dv(32), 4)
             vtt(T.ae[:], T.nb[:], T.Ec[:], ALU.mult, ["nb", "Ec"], ["ae"], 64)
             mm([(pR, T["U%d" % e][:], T.nb[:, e:32:2]) for e in range(2)] + [(pR, T["S%d" % e][:], T.ae[:, e:32:2]) for e in range(2)]
                + [(pR, T.I32[:], T.J[:, 0:16]), (pR, T.nI32[:], T.Sc[:, 0:16])],
-               ["U0", "U1", "S0", "S1", "nb", "I32", "J", "ae", "nI32", "Sc"], ["pR"], 7)
-            vcp(T.PI[:], pR, ["pR"], ["PI"], 16, 7)
-            mm([(ps[7][:, 256:512], T.I16[:], T.N5[:, 0:A:2]), (ps[7][:, 256:512], T.Sh2[:], T.N5[:, 1:A:2])],
-               ["I16", "Sh2", nA], ["pp"], 7)
-            act(T.pk2[:], ps[7][:, 256:512], ID, ["pp"], ["pk2"], S, bank=7)
-            vcp(T.CV[:].indirect(T.PI[:]), T.pk2[:], ["PI", "pk2"], ["CV"], S * C["SC"] + 30)
+               ["U0", "U1", "S0", "S1", "nb", "I32", "J", "ae", "nI32", "Sc"], ["pR"], 4)
+            vcp(T.PI[:], pR, ["pR"], ["PI"], 16, 4)
+            mm([(ps[5][:, 0:S], T.I16[:], T.N5[:, 0:A:2]), (ps[5][:, 0:S], T.Sh2[:], T.N5[:, 1:A:2])],
+               ["I16", "Sh2", nA], ["b5"], 5)
+            act(T.pk2[:], ps[5][:, 0:S], ID, ["b5"], ["pk2"], S, bank=5)
+            vcp(T.CV[:].indirect(T.PI[:]), T.pk2[:], ["PI", "pk2"], ["CV"], S * C["SC"] + 55)
             mm([(pk, T["BigM" if i % 2 else "BigN"][:, 15 - i:143 - i], T.CV[:, i // 2:128:8]) for i in range(16)],
-               ["CV", "BigN", "BigM"], ["pk"], 7)
-            vcp(T.TI[:], pk, ["pk"], ["TI"], 16, 7)
-            agather(snd, 0, Wc, T.TI, 0, 16, WK + ["TI"], "snd%d" % r, bias=-M)
+               ["CV", "BigN", "BigM"], ["pk"], 4)
+            vcp(T.TI[:], pk, ["pk"], ["TI"], 16, 4)
+            agather(snd, 0, Wc, T.TI, 0, 16, WK + ["TI"], "snd%d" % r, 1, O["hops"][2], 0.5 - E)
             act(snd[:, S:S + 1], T.Sc[:, 15:16], ID, ["Sc"], ["sndc%d" % r], 1, bias=float(A), scale=-2.0)
 
             def send(snd=snd, land=land, r=r):
@@ -349,66 +407,39 @@ def build(g, core, T, topo, C, O):
                                                 remote_sem=T.sem["arr%d" % r], src=snd[:], dst=land[:, d * SW:(d + 1) * SW]))
                 g.remote_dma_fused(tr, local_sem=T.sem.sent)
                 return None
-            op("g", send, ["snd%d_0" % r, "sndc%d" % r], ["land%d" % r], 1.0, None, "rem", ("arr%d" % r, 12), 128 * 528 * 3)
-        steps(r, [2, 3, 4])
-        for h in range(2):
-            if cvk[h] is None:
-                a, key, o = xi(r + 1, 0, h)
-                for k in range(2):
-                    wd = slice(h * H + k * 512, h * H + (k + 1) * 512)
-                    vtt(T.db[:, wd], Wc.indirect(T.XI[:, o + 32 * k:o + 32 * k + 32]), T.Z[:, wd], ALU.subtract,
-                        WK + [key, ZK[h][k]], [DK[h][k]], 512 * C["G"] + 30)
+            op("g", send, ["snd%d_0" % r, "sndc%d" % r], ["land%d" % r], 1.0, None, "rem", ("arr%d" % r, 12), 128 * 528 * 6)
+        steps(r, [2, 3, 4], cvk)
         if not last:
-            pd = ps[6][:, 0:SW]
+            pd = ps[5][:, 0:SW]
             mm([(pd, T.Psh[:, ((d - r) % 3) * 128:((d - r) % 3) * 128 + 128], land[:, d * SW:(d + 1) * SW]) for d in range(3)],
-               ["Psh", "land%d" % r], ["pd"], 6)
-            act(T.arr[:], ps[6][:, 0:S], ID, ["pd"], ["arr"], S, bias=M, bank=6)
-            vtt(T.nmin[:, 0:1], ps[6][:, S:S + 1], snd[:, S:S + 1], ALU.min, ["pd", "sndc%d" % r], ["nmin"], 1, 6)
+               ["Psh", "land%d" % r], ["b5"], 5)
+            addc(O["hops"][3], T.arr[:], ps[5][:, 0:S], E - 0.5, ["b5"], ["arr"], S, 5)
+            vtt(T.nmin[:, 0:1], ps[5][:, S:S + 1], snd[:, S:S + 1], ALU.min, ["b5", "sndc%d" % r], ["nmin"], 1, 5)
             vts(T.q1[:], T.J[:, 0:16], T.nmin[:, 0:1], K, GE, ALU.mult, ["J", "nmin"], ["q1"], 16)
-            vtt(T.q2[:], pk, T.q1[:], ALU.max, ["pk", "q1"], ["q2"], 16, 7)
+            vtt(T.q2[:], pk, T.q1[:], ALU.max, ["pk", "q1"], ["q2"], 16, 4)
             vtt(T.q3[:], T.q2[:], T.Dk[:], ALU.min, ["q2", "Dk"], ["q3"], 32)
             vcp(T.DI[:], T.q3[:], ["q3"], ["DI"], 16)
-            vcp(W[:].indirect(T.DI[:]), T.arr[:], ["DI", "arr"], WK, S * C["SC"] + 30)
-        for h in range(2):
-            for k in range(2):
-                o = h * H + k * 512
-                b = 4 + k
-                if cvk[h] is None:
-                    act(T.zbf[:, o:o + 512], T.db[:, o:o + 512], ACT.Abs, [DK[h][k]], [FK[h][k]], 512)
-                else:
-                    mm([(ps[b][:], T.I16[:], T.cv[:, o:o + 512]), (ps[b][:], T.nI32[:], T.Z[:, o:o + 512])],
-                       ["I16", "nI32", cvk[h][k], ZK[h][k]], ["pz%d" % b], b)
-                    act(T.zbf[:, o:o + 512], ps[b][:], ACT.Abs, ["pz%d" % b], [FK[h][k]], 512, bias=M, bank=b)
-                if last:
-                    dma("s", T.yz[:, o:o + 512], T.zbf[:, o:o + 512], [FK[h][k]], ["yz%d" % o], 128 * 1024)
-                else:
-                    addc(O["addm"][k], T.Z[:, o:o + 512], T.zbf[:, o:o + 512], M, [FK[h][k]], [ZK[h][k]], 512)
+            vcp(WZ[:, H:H + V + S].indirect(T.DI[:]), T.arr[:], ["DI", "arr"], WK + ["dump"], S * C["SC"] + 55)
     return ops
 
 
 def depend(ops):
-    lastw, readers, bankl, prevq = {}, {}, {}, {}
+    lastw, readers, prevq = {}, {}, {}
     for i, o in enumerate(ops):
         d = set()
-        for k in o["r"] + o.get("after", []):
+        for k in o["r"]:
             if k in lastw:
                 d.add(lastw[k])
-        for k in o["w"]:
+        for k in o["w"] + o.get("after", []):
             if k in lastw:
                 d.add(lastw[k])
             d.update(readers.get(k, []))
-        b = o["bank"]
-        if b is not None:
-            run = bankl.get(b)
-            if run is None or run[0] != o["eng"]:
-                run = [o["eng"], [], run[1] if run else []]
-                bankl[b] = run
-            d.update(run[2])
-            run[1].append(i)
         d.discard(i)
         o["dep"] = sorted(d)
-        o["prev"] = prevq.get(o["eng"]) if o["eng"] in "sg" else None
-        prevq[o["eng"]] = i
+        o["prev"] = None
+        if o["eng"] == "s" and o["w"][0][:2] in ("nx", "zf", "CT", "NT") and o["w"][0][:3] != "NTc":
+            o["prev"] = prevq.get("s")
+            prevq["s"] = i
         for k in o["r"]:
             readers.setdefault(k, []).append(i)
         for k in o["w"]:
@@ -417,109 +448,247 @@ def depend(ops):
     return ops
 
 
-def listsched(ops, C, succ, left0, pr, look):
-    n = len(ops)
+def listsched(P, pr, eager):
+    eng, bank, dur, isd, tb, succ, left0, sy, d0 = P
+    n = len(eng)
     left = list(left0)
-    free = {e: 0.0 for e in "vapgs"}
-    ready = {e: [] for e in "vapgs"}
-    fin, start, rt = [0.0] * n, [0.0] * n, [0.0] * n
-    pipe, sy, d0, rate = 0.0, C["sync"], C["dma0"], C["rate"]
-    cand, seq = {}, []
+    free, ready, cand = [0.0] * 5, [[] for _ in range(5)], [None] * 5
+    held = [[0.0] * 3 for _ in range(8)]
+    rt, start = [0.0] * n, [0.0] * n
+    pipe, end, seq = 0.0, 0.0, []
     for i in range(n):
         if left[i] == 0:
-            ready[ops[i]["eng"]].append(i)
+            ready[eng[i]].append(i)
     for _ in range(n):
         best = None
-        for e in "vapgs":
-            if e not in cand:
-                c = ready[e]
-                if not c:
+        for e in range(5):
+            if cand[e] is None:
+                if not ready[e]:
                     continue
-                t0 = max(free[e], min(rt[i] for i in c)) + look
-                i = max((i for i in c if rt[i] <= t0), key=lambda i: pr[i])
-                cand[e] = (max(free[e], rt[i]), i)
+                f, top = free[e], -1e9
+                for i in ready[e]:
+                    t, b = rt[i], bank[i]
+                    if b is not None and held[b][e] > t:
+                        t = held[b][e]
+                    if t < f:
+                        t = f
+                    if pr[i] - eager * t > top:
+                        top, cand[e] = pr[i] - eager * t, (t, i)
             if best is None or cand[e][0] < best[0]:
                 best = cand[e]
         t, i = best
-        o = ops[i]
-        e = o["eng"]
+        e, b = eng[i], bank[i]
         ready[e].remove(i)
         seq.append(i)
         start[i] = t
-        free[e] = fin[i] = t + o["dur"]
-        del cand[e]
-        if o["kind"] != "c":
-            pipe = max(pipe, free[e] + d0 * 0.7) + o["nb"] / rate
-            fin[i] = pipe + d0 * 0.3
+        free[e] = f = t + dur[i]
+        cand[e] = None
+        if b is not None:
+            for x in (0, 1, 2):
+                if x != e:
+                    held[b][x] = f + sy
+                    if cand[x] is not None and bank[cand[x][1]] == b:
+                        cand[x] = None
+        if isd[i]:
+            pipe = max(pipe, f + d0 * 0.7) + tb[i]
+            f = pipe + d0 * 0.3
+        end = max(end, f)
         for j, real in succ[i]:
-            if real and fin[i] + sy > rt[j]:
-                rt[j] = fin[i] + sy
+            if real and f + sy > rt[j]:
+                rt[j] = f + sy
             left[j] -= 1
             if left[j] == 0:
-                ready[ops[j]["eng"]].append(j)
-                cand.pop(ops[j]["eng"], None)
-    return seq, start, max(fin)
+                ready[eng[j]].append(j)
+                cand[eng[j]] = None
+    return seq, start, end
 
 
-def replay(ops, C, seq):
-    free = {e: 0.0 for e in "vapgs"}
-    fin = [0.0] * len(ops)
-    pipe, sy, d0, rate = 0.0, C["sync"], C["dma0"], C["rate"]
+def replay(P, dep, seq):
+    eng, bank, dur, isd, tb, succ, left0, sy, d0 = P
+    free = [0.0] * 5
+    held = [[0.0] * 3 for _ in range(8)]
+    fin = [0.0] * len(eng)
+    pipe = 0.0
     for i in seq:
-        o = ops[i]
-        t = free[o["eng"]]
-        for j in o["dep"]:
-            if fin[j] + sy > t:
-                t = fin[j] + sy
-        free[o["eng"]] = fin[i] = t + o["dur"]
-        if o["kind"] != "c":
-            pipe = max(pipe, fin[i] + d0 * 0.7) + o["nb"] / rate
-            fin[i] = pipe + d0 * 0.3
+        e, b = eng[i], bank[i]
+        t = free[e]
+        for j in dep[i]:
+            if fin[j] > t:
+                t = fin[j]
+        if b is not None:
+            t = max(t, held[b][e]) + dur[i]
+            for x in (0, 1, 2):
+                if x != e:
+                    held[b][x] = t + sy
+        else:
+            t += dur[i]
+        free[e] = t
+        if isd[i]:
+            pipe = max(pipe, t + d0 * 0.7) + tb[i]
+            t = pipe + d0 * 0.3
+        fin[i] = t + sy
     return max(fin)
 
 
 def plan(mk, C, O, vary):
     ops = mk(C)
-    alt = [(mk(dict(C, **m)), dict(C, **m)) for m in vary]
     n = len(ops)
     succ, left = [[] for _ in range(n)], [0] * n
     for i, o in enumerate(ops):
         for j in sorted(set(o["dep"] + ([o["prev"]] if o["prev"] is not None else []))):
             succ[j].append((i, j in o["dep"]))
             left[i] += 1
+
+    def table(ops, C):
+        return (["vapgs".index(o["eng"]) for o in ops], [o["bank"] for o in ops], [o["dur"] for o in ops],
+                [o["kind"] != "c" for o in ops], [o["nb"] / C["rate"] for o in ops], succ, left, C["sync"], C["dma0"])
+    P = table(ops, C)
+    alt = [table(mk(dict(C, **m)), dict(C, **m)) for m in vary]
+    dep = [o["dep"] for o in ops]
     pr = np.zeros(n)
+    t0, pace, gap, end = O["pace"]
     for i in range(n - 1, -1, -1):
         o = ops[i]
-        pr[i] = o["dur"] + (0.0 if o["kind"] == "c" else C["dma0"] + o["nb"] / C["rate"]) \
-            + max([pr[j] + C["sync"] for j, _ in succ[i]] + [0.0])
+        late = min([-pr[j] - (C["sync"] if ops[j]["eng"] in ("p", o["eng"]) else O["hop"]) for j, _ in succ[i]] + [end]) - o["dur"] - o.get("spare", 0.0) \
+            - (0.0 if o["kind"] == "c" else C["dma0"] + o["nb"] / C["rate"])
+        if "due" in o:
+            r, s, k = o["due"]
+            late = min(late, t0 + (4 * pace + gap) * r + pace * (s - 1 + (k // 2) * O["skew"] + (k % 2) / 4))
+        pr[i] = -late
 
-    def score(p):
-        seq, start, end = listsched(ops, C, succ, left, p.tolist(), O["look"])
-        return np.array([end] + [replay(o2, C2, seq) for o2, C2 in alt]), seq, np.array(start)
     rs = np.random.RandomState(O["seed"])
-    a0, seq, st = score(pr)
+    seq, st, end = listsched(P, pr.tolist(), O["eager"])
+    a0 = np.array([end] + [replay(x, dep, seq) for x in alt])
     w = np.array([2.0] + [1.0] * len(alt)) / a0
     w = w / np.dot(a0, w) * a0[0]
     cur = best = float(np.dot(a0, w))
-    out = (seq, a0, st)
+    st, out, cur0 = np.array(st), (seq, a0), end
     for it in range(O["iters"]):
         p = pr.copy()
         k = rs.randint(4)
         if k == 0:
             a = rs.randint(n)
-            p[a:a + rs.randint(1, 40)] += rs.normal(0, 4.0)
+            p[a:a + rs.randint(1, 40)] += rs.normal(0, 3.0)
         elif k == 2:
-            p[rs.randint(n, size=3)] += rs.normal(0, 3.0, 3)
+            p[rs.randint(n, size=3)] += rs.normal(0, 2.0, 3)
         else:
             t = rs.rand() * st.max()
             m = (abs(st - t) < 3) & (rs.rand(n) < 0.3) if k == 1 else abs(st - t) < 6
-            p[m] += rs.normal(0, 2.0 if k == 1 else 0.5, m.sum())
-        a, seq, start = score(p)
+            p[m] += rs.normal(0, 1.5 if k == 1 else 0.4, m.sum())
+        seq, start, end = listsched(P, p.tolist(), O["eager"])
+        slack = O["temp"] * (1 - it / O["iters"]) * rs.exponential()
+        if end > cur0 + 1.5 + slack:
+            continue
+        a = np.array([end] + [replay(x, dep, seq) for x in alt])
         s = float(np.dot(a, w))
-        if s <= cur + O["temp"] * (1 - it / O["iters"]) * rs.rand():
-            cur, pr, st = s, p, start
+        if s <= cur + slack:
+            cur, cur0, pr, st = s, end, p, np.array(start)
             if s < best:
-                best, out = s, (seq, a, start)
+                best, out = s, (seq, a)
+    return out
+
+
+def polish(mk, C, O, vary, seq):
+    ops = mk(C)
+    n = len(ops)
+    eng = ["vapgs".index(o["eng"]) for o in ops]
+    bank = [o["bank"] for o in ops]
+    dep = [o["dep"] for o in ops]
+    pre = [set(o["dep"] + ([o["prev"]] if o["prev"] is not None else [])) for o in ops]
+    isd = [o["kind"] != "c" for o in ops]
+    var = []
+    for m in [{}] + vary:
+        C2 = dict(C, **m)
+        o2 = mk(C2)
+        var.append(([o["dur"] for o in o2], [o["nb"] / C2["rate"] for o in o2], C2["sync"], C2["dma0"]))
+
+    def run(seq, v):
+        dur, tb, sy, d0 = v
+        free, who = [0.0] * 5, [-1] * 5
+        held = [[0.0, 0.0, 0.0, -1, -1, -1] for _ in range(8)]
+        fin, why, res = [0.0] * n, [-1] * n, [True] * n
+        pipe = 0.0
+        for i in seq:
+            e = eng[i]
+            t, y, q = free[e], who[e], True
+            for j in dep[i]:
+                if fin[j] > t:
+                    t, y, q = fin[j], j, False
+            b = bank[i]
+            if b is not None:
+                hb = held[b]
+                if hb[e] > t:
+                    t, y, q = hb[e], hb[3 + e], True
+                t += dur[i]
+                for x in (0, 1, 2):
+                    if x != e:
+                        hb[x], hb[3 + x] = t + sy, i
+            else:
+                t += dur[i]
+            free[e], who[e], why[i], res[i] = t, i, y, q
+            if isd[i]:
+                pipe = max(pipe, t + d0 * 0.7) + tb[i]
+                t = pipe + d0 * 0.3
+            fin[i] = t + sy
+        end = max(fin)
+        i, arcs = fin.index(end), []
+        while i >= 0:
+            if res[i] and why[i] >= 0 and why[i] not in pre[i]:
+                arcs.append((why[i], i))
+            i = why[i]
+        return end, arcs
+
+    def swap(seq, j, i):
+        a, b = seq.index(j), seq.index(i)
+        need, wait, engs, banks = [i], set(pre[i]), set(), set()
+        for x in seq[b - 1:a:-1]:
+            if x in wait or eng[x] in engs or (bank[x], eng[x]) in banks or eng[x] == eng[i] \
+                    or (bank[x] is not None and bank[x] == bank[i]):
+                need.append(x)
+                wait |= pre[x]
+                engs.add(eng[x])
+                if bank[x] is not None:
+                    banks.update((bank[x], e) for e in range(3) if e != eng[x])
+        if j in wait or eng[j] in engs or (bank[j], eng[j]) in banks:
+            return None
+        s = set(need)
+        return seq[:a] + need[::-1] + [x for x in seq[a:b] if x not in s] + seq[b + 1:]
+
+    res = [run(seq, v) for v in var]
+    w = np.array([2.0] + [1.0] * len(vary)) / np.array([r[0] for r in res])
+    w = (w / np.dot(w, [r[0] for r in res]) * res[0][0]).tolist()
+    total = lambda res: sum(a * r[0] for a, r in zip(w, res))
+    cur = best = total(res)
+    out = (list(seq), np.array([r[0] for r in res]))
+    rs = np.random.RandomState(O["seed"])
+    for it in range(O["moves"]):
+        arcs = res[rs.randint(len(res))][1]
+        if not arcs:
+            continue
+        j, i = arcs[rs.randint(len(arcs))]
+        s2 = swap(seq, j, i)
+        for _ in range(rs.geometric(O["far"]) - 1):
+            if s2 is None:
+                break
+            p = s2.index(i) - 1
+            while p >= 0 and eng[s2[p]] != eng[i]:
+                p -= 1
+            s3 = swap(s2, s2[p], i) if p >= 0 and s2[p] not in pre[i] else None
+            if s3 is None:
+                break
+            s2 = s3
+        if s2 is None:
+            continue
+        slack = O["heat"] * (1 - it / O["moves"]) * rs.exponential()
+        r0 = run(s2, var[0])
+        if r0[0] > res[0][0] + 1.0 + 2 * slack:
+            continue
+        r2 = [r0] + [run(s2, v) for v in var[1:]]
+        s = total(r2)
+        if s <= cur + slack:
+            cur, seq, res = s, s2, r2
+            if s < best:
+                best, out = s, (list(seq), np.array([r[0] for r in res]))
     return out
 
 
@@ -528,43 +697,43 @@ def rank_program(g, core, T, topo):
         return
     mk = lambda C: depend(build(g, core, T, topo, C, OPT))
     if "seq" not in PLAN:
-        PLAN["seq"] = plan(mk, COST, OPT, VARY)[0]
+        PLAN["seq"], PLAN["est"] = polish(mk, COST, OPT, VARY, plan(mk, COST, OPT, VARY)[0])
     ops = mk(COST)
-    order = {e: [i for i in PLAN["seq"] if ops[i]["eng"] == e] for e in "vapgs"}
+    seq = PLAN["seq"]
     queue = {"v": g.vector, "a": g.scalar, "p": g.tensor, "g": g, "s": g.sync}
-    final = {}
-    nd = 0
-    for e in "vapgs":
-        cnt = 0
-        for i in order[e]:
-            o = ops[i]
-            if o["kind"] == "c":
-                cnt += 1
-                o["sig"] = ("s" + e, cnt)
-            elif o["kind"] == "dma":
-                o["sig"] = ("d%d" % nd, 16)
-                nd += 1
-            else:
-                o["sig"] = o["ext"]
-                final["sent"] = final.get("sent", 0) + 12
-            final[o["sig"][0]] = o["sig"][1]
-    for e in "vapgs":
-        seen = {}
-        q = queue[e]
-        for i in order[e]:
-            o = ops[i]
-            need = {}
-            for j in o["dep"]:
-                s, v = ops[j]["sig"]
-                need[s] = max(need.get(s, 0), v)
-            for s in sorted(need):
-                if need[s] > seen.get(s, 0):
-                    q.wait_ge(T.sem[s], need[s])
-                    seen[s] = need[s]
-            ins = o["fn"]()
-            if o["kind"] != "rem":
-                ins.then_inc(T.sem[o["sig"][0]], 1 if o["kind"] == "c" else 16)
-        if e == "g":
-            for s in sorted(final):
-                if final[s] > seen.get(s, 0):
-                    q.wait_ge(T.sem[s], final[s])
+    final, cnt, nd = {}, {e: 0 for e in "vapg"}, 0
+    last = {b: {} for b in range(8)}
+    for at, i in enumerate(seq):
+        o = ops[i]
+        o["at"] = at
+        if o["bank"] is not None:
+            o["dep"] = o["dep"] + [j for e, j in last[o["bank"]].items() if e != o["eng"]]
+            last[o["bank"]][o["eng"]] = i
+        if o["kind"] == "c":
+            cnt[o["eng"]] += 1
+            o["sig"] = ("s" + o["eng"], cnt[o["eng"]])
+        elif o["kind"] == "dma":
+            o["sig"] = ("d%d" % nd, 16)
+            nd += 1
+        else:
+            o["sig"] = o["ext"]
+            final["sent"] = final.get("sent", 0) + 12
+        final[o["sig"][0]] = o["sig"][1]
+    seen = {e: {} for e in queue}
+    for i in seq:
+        o = ops[i]
+        know = seen[o["eng"]]
+        for j in sorted(o["dep"], key=lambda j: -ops[j]["at"]):
+            s, v = ops[j]["sig"]
+            if v > know.get(s, 0):
+                queue[o["eng"]].wait_ge(T.sem[s], v)
+                know[s] = v
+                for s2, v2 in ops[j]["knew"].items():
+                    know[s2] = max(know.get(s2, 0), v2)
+        o["knew"] = dict(know) if o["kind"] != "rem" else {}
+        ins = o["fn"]()
+        if o["kind"] != "rem":
+            ins.then_inc(T.sem[o["sig"][0]], 1 if o["kind"] == "c" else 16)
+    for s in sorted(final):
+        if final[s] > seen["g"].get(s, 0):
+            g.wait_ge(T.sem[s], final[s])

import numpy as np
from concourse.bass import DstId, RemoteDMATransfer
from concourse.mybir import dt, AluOpType, AxisListType, ActivationFunctionType

V, L, A, S, RO = 8192, 2048, 512, 256, 3
H = L // 2
HW = H // 16
B = 512
E = 1024.0
K = 32768.0
XO = 16384.0
SW = 264
NDMA = 100

SCRATCH = {}
for _t, _l in (("float32", dict(WZ=L + V + S, Zi=L, Y=V + A, v32=A, xf=256, tm=128, prod=512, uf=32, upk=32, tc=32, Sc=32, ae=32, arr=S,
                                nmin=4, q1=16, q2=16, q3=16, wf=4, one32=128, I32=128, nI32=128, Pp=128, pf=4, J0=64, J=64,
                                JE=128, JA=128, S0=128, S1=128, Dc=32, Ec=32, Dk=16)),
               ("float16", dict(Z16=L)),
               ("bfloat16", dict(NT=V + A, CT=V, Nc=L, cmpb=L, zbf=L, cv=L, Nw=L, N5=L, EQ=512, hT=64, OH=32 * 192,
                                 Hs=512, aw=A, nb=32, CV=S, snd0=SW, snd1=SW, land0=3 * SW, land1=3 * SW, hb=512, lb=512,
                                 one16=144, BigN=144, BigV=144, BigC=144, BigP=144, SelT=16, ioA=64, ioB=128,
                                 I16=128, nI16=128, Ih=128, Blk=128, U0=128, U1=128, Sh2=128, BigM=144, pk2=S, Psh=384,
                                 BigK=144, KI=128)),
               ("int32", dict(ci=128, cj=128, nxi=512, nxl=512, curi=128, wi=4, wj=4, pi=4, pj=4)),
               ("uint16", dict(XI=1280, UI=128, I2=128, CI=32, PI=16, TI=16, DI=16))):
    for _n, _c in _l.items():
        SCRATCH[_n] = ("sbuf", [128, _c], _t)
for _b in range(8):
    SCRATCH["ps%d" % _b] = ("psum", [128, 512], "float32")
SEMAPHORES = ["sv", "sa", "sp", "sg", "arr0", "arr1", "sent"] + ["d%d" % _i for _i in range(NDMA)]

COST = {"cyc": 0.00084, "pe": 0.0005, "G": 1.5, "SC": 3.6, "sync": 0.11, "fix": 0.005, "dma0": 2.0, "rate": 380000.0}
VARY = [{"G": 1.1, "SC": 2.0}, {"G": 1.9, "SC": 5.0, "cyc": 0.0011}, {"sync": 0.22, "fix": 0.03}, {"pe": 0.00083}]
OPT = {"how": [["eeee", "eeae"], ["eaee", "eeae"], ["eaee", "eeae"]], "chain": ["vavaaaaa", "aaaaaaaa", "aaaaaaaa"], "twin": ["g" * 16] * 3, "conv": "aaavavav",
       "sub": (1, 1), "f16": True, "csub": 1, "fill": 2560, "pre": 2,
       "pace": (13, 7.8, 1, 112), "skew": 0.5, "hop": 0.8, "hops": "vava", "spare": 0.6, "eager": 200.0, "seed": 0, "iters": 3000, "temp": 0.15,
       "moves": 1500, "heat": 0.1, "far": 0.6}
ALU = AluOpType
ACT = ActivationFunctionType
PLAN = {}


def build(g, core, T, topo, C, O):
    rank = T.rank_of(core)
    N = len(T.cores)
    ops = []
    cyc = C["cyc"]
    ID = ACT.Identity

    def op(eng, fn, r, w, dur, bank=None, kind="c", ext=None, nbytes=0):
        ops.append({"eng": eng, "fn": fn, "r": list(r), "w": list(w), "dur": dur, "bank": bank, "kind": kind,
                    "ext": ext, "nb": nbytes})

    def after(keys):
        ops[-1]["after"] = list(keys)

    def dv(n):
        return max(64, n) * cyc + C["fix"]

    def vts(out, in0, s1, s2, o0, o1, r, w, n, bank=None):
        if o1 is None:
            op("v", lambda: g.vector.tensor_scalar(out, in0, s1, None, o0), r, w, dv(n), bank)
        else:
            op("v", lambda: g.vector.tensor_scalar(out, in0, s1, s2, o0, o1), r, w, dv(n), bank)

    def vtt(out, in0, in1, o, r, w, n, bank=None):
        op("v", lambda: g.vector.tensor_tensor(out, in0, in1, o), r, w, dv(n), bank)

    def vcp(out, in_, r, w, n, bank=None):
        op("v", lambda: g.vector.tensor_copy(out, in_), r, w, dv(n), bank)

    def vset(out, w, n, c=0.0):
        op("v", lambda: g.vector.memset(out, c), [], w, dv(n))

    def act(out, in_, f, r, w, n, bias=0.0, scale=1.0, bank=None):
        op("a", lambda: g.scalar.activation(out, in_, f, bias=bias, scale=scale), r, w, dv(n), bank)

    def addc(e, out, in_, c, r, w, n, bank=None):
        if e == "a":
            act(out, in_, ID, r, w, n, bias=c, bank=bank)
        else:
            vts(out, in_, c, None, ALU.add, None, r, w, n, bank)

    def mm(lst, r, w, bank, how="group"):
        def fn():
            ins = None
            for k, (o, l, x) in enumerate(lst):
                ins = g.tensor.matmul(o, l, x, how == "each" or (how in ("group", "open") and k == 0),
                                      how == "each" or (how in ("group", "close") and k == len(lst) - 1))
            return ins
        cy = sum(max(min(64, l.shape[1]), x.shape[1]) * (4 if str(x.dtype).find("32") >= 0 else 1) for (o, l, x) in lst)
        op("p", fn, r, w, cy * C["pe"] + C["fix"], bank)

    def dma(q, out, in_, r, w, nbytes, **kw):
        e = {"s": g.sync, "a": g.scalar, "g": g}[q]
        op(q, lambda: e.dma_start(out, in_, **kw), r, w, 0.1 if q != "g" else 1.0, None, "dma", None, nbytes)

    def gio(name, pat, base, cm, out=None):
        o = T[name][:] if out is None else out
        kw = {} if name == "pi" else {"allow_small_or_imprecise_dtypes": True}
        op("g", lambda: g.iota(o, pat, base, cm, **kw), [], [name], 0.13 + 2 * o.shape[1] * cyc)

    def gsel(name, src, pat, cmp, base, cm, out=None):
        o = T[name][:] if out is None else out
        op("g", lambda: g.affine_select(o, T[src][:, 0:o.shape[1]], pat, cmp, 0.0, base, cm), [src], [name],
           0.17 + 2 * o.shape[1] * cyc)

    ps = [T["ps%d" % b] for b in range(8)]
    WZ = T.WZ
    Wc = WZ[:, H:H + V]
    NCC = 8
    CW = V // NCC
    WK = ["W%d" % k for k in range(NCC)]
    NK = ["NTh", "NTl"] + ["NTc%d" % q for q in range(4)]
    GE, EQL = ALU.is_ge, ALU.is_equal
    PX, PC = 0, 256

    def xi(r, s, h):
        o = ((r % 2) * 5 + s) * 128 + h * HW
        return T.XI[:, o:o + HW], "xi%d_%d_%d" % (r % 2, s, h), o

    def zat(k):
        o = (k // 2) * (H + V + S) + (k % 2) * B
        return WZ[:, o:o + B]

    dma("s", T.nxi[:], T.nx[:], [], ["nxi"], 128 * 2048)
    dma("a", T.curi[:], T.cur[:], [], ["curi"], 128 * 512)
    dma("a", T.wi[:, 0:1], T.wt[:], [], ["wi"], 128 * 64)
    dma("s", T.zbf[:], T.z0[:], [], ["zf%d" % k for k in range(4)], 128 * 4096)
    F = O["fill"]
    vset(T.NT[:, 0:F], ["NT0"], F // 2)
    vset(T.NT[:, 2 * F:V + A], ["NT2"], (V + A - 2 * F) // 2)
    act(T.NT[:, F:2 * F], T.NT[:, 0:F], ID, ["NT0"], ["NT1"], F)
    vset(WZ[:, H + V:H + V + S], ["dump"], S)

    def load(k):
        dma("s", T.CT[:, k * CW:(k + 1) * CW], T.cards[:, k * CW:(k + 1) * CW], [], ["CT%d" % k], 128 * CW * 2)
        addc(O["conv"][k], WZ[:, H + k * CW:H + (k + 1) * CW], T.CT[:, k * CW:(k + 1) * CW], E - 0.5, ["CT%d" % k], [WK[k]], CW)

    for k in range(O["pre"]):
        load(k)
    vts(T.nxl[:], T.nxi[:], 127, None, ALU.bitwise_and, None, ["nxi"], ["nxl"], 512)
    vtt(T.hb[:], T.nxi[:], T.nxl[:], ALU.subtract, ["nxi", "nxl"], ["hb"], 1024)
    vcp(T.lb[:], T.nxl[:], ["nxl"], ["lb"], 512)
    dma("s", T.NT[0:128:16, 0:V], T.hb[:], ["hb"], ["NTh"], 128 * 1024)
    after(["NT0", "NT1", "NT2"])
    dma("s", T.NT[1:128:16, 0:V], T.lb[:], ["lb"], ["NTl"], 128 * 1024)
    after(["NT0", "NT1", "NT2"])
    for k in range(O["pre"], NCC):
        load(k)
    for h in range(2):
        a, key, o = xi(0, 0, h)
        vcp(a, T.curi[:, h * HW:(h + 1) * HW], ["curi"], [key], HW)

    gio("one16", [[0, 144]], 1, 0)
    gsel("BigV", "one16", [[-16, 9], [0, 16]], GE, 0, 1)
    gsel("BigN", "BigV", [[16, 9], [1000, 16]], GE, 1 - 15000, -1)
    gsel("BigV", "BigV", [[16, 9], [1000, 16]], GE, 15 - 15000, -1)
    gsel("I16", "one16", [[-1, 128]], EQL, 0, 1)
    gio("pi", [[0, 1]], 0, 1, T.pi[:, 0:1])
    gio("J0", [[16, 64]], 0, 0)
    gio("one32", [[0, 128]], 1, 0)
    gsel("I32", "one32", [[-1, 128]], EQL, 0, 1)
    gsel("SelT", "one16", [[-16, 8], [-1, 2]], EQL, 0, 1)
    gio("ioA", [[128, 64]], 0, 0)
    gio("ioB", [[1, 128]], 0, 0)
    gsel("Pp", "one32", [[-2, 64], [1, 2]], EQL, -1, 1)
    gio("BigP", [[0, 144]], int(K), 0)
    gsel("BigP", "BigP", [[-16, 9], [0, 16]], EQL, 12, 1)
    gsel("BigP", "BigP", [[0, 9], [-1, 16]], GE, 1, 0)
    gsel("Blk", "one16", [[-16, 8], [0, 16]], GE, 0, 1)
    gsel("Blk", "Blk", [[16, 8], [0, 16]], GE, 15, -1)
    for e in range(2):
        gsel("U%d" % e, "Blk", [[-16, 8], [-2, 16]], GE, 16 * e, 1)
        gsel("S%d" % e, "one32", [[-16, 8], [0, 16]], GE, 0, 1)
        gsel("S%d" % e, "S%d" % e, [[16, 8], [0, 16]], GE, 15, -1)
        gsel("S%d" % e, "S%d" % e, [[-16, 8], [-2, 16]], EQL, 16 * e, 1)
    gsel("Sh2", "one16", [[-1, 128]], EQL, 2, 1)
    gsel("BigM", "one16", [[-16, 9], [0, 16]], GE, -2, 1)
    gsel("BigM", "BigM", [[16, 9], [1000, 16]], GE, 3 - 15000, -1)
    gio("Psh", [[0, 384]], 0, 0)
    for gr in range(8):
        o = (gr % 3) * 128 + ((gr + 1) % 8) * 16
        gsel("Psh", "one16", [[-1, 16]], EQL, -16 * gr, 1, T.Psh[:, o:o + 16])
    gio("sndc0", [[0, SW - S]], 0, 0, T.snd0[:, S:SW])
    gio("sndc1", [[0, SW - S]], 0, 0, T.snd1[:, S:SW])

    vts(T.wj[:, 0:1], T.wi[:, 0:1], 3, None, ALU.bitwise_and, None, ["wi"], ["wj"], 1)
    vcp(T.wf[:, 0:1], T.wj[:, 0:1], ["wj"], ["wf"], 1)
    vts(T.BigC[:], T.BigV[:], T.wf[:, 0:1], None, ALU.mult, None, ["BigV", "wf"], ["BigC"], 72)
    vts(T.pj[:, 0:1], T.pi[:, 0:1], 15, None, ALU.bitwise_and, None, ["pi"], ["pj"], 1)
    vcp(T.pf[:, 0:1], T.pj[:, 0:1], ["pj"], ["pf"], 1)
    for name, src, n, scale in (("nI16", "I16", 128, -1.0), ("Ih", "I16", 128, 0.5), ("KI", "I16", 128, 16 * K),
                                ("nI32", "I32", 128, -1.0), ("BigK", "BigV", 144, -K)):
        act(T[name][:], T[src][:], ID, [src], [name], n, scale=scale)
    act(T.J[:], T.J0[:], ID, ["J0", "pf"], ["J"], 64, bias=T.pf[:, 0:1])
    for name, lo in (("JE", 9 * K), ("JA", K)):
        if name == "JE" or "a" in str(O["how"]):
            act(T[name][:, 0:HW], T.J[:], ID, ["J"], [name + "0"], HW, bias=XO - lo, scale=-1.0)
            act(T[name][:, HW:2 * HW], T.J[:], ID, ["J"], [name + "1"], HW, bias=XO - lo + V + S)
    act(T.Dc[:], T.J[:, 0:32], ID, ["J"], ["Dc"], 32, bias=V + 2.5 * K)
    act(T.Ec[:], T.J[:, 0:32], ID, ["J"], ["Ec"], 32, bias=510.0, scale=-1.0)
    act(T.Dk[:], T.J[:, 0:16], ID, ["J"], ["Dk"], 16, bias=float(V))

    def agather(out, oo, win, off, fo, ncol, r, w, sub=1, eng="a", bias=0.0):
        st = ncol // sub
        for k in range(sub):
            o = out[:, oo + 16 * k * st:oo + 16 * (k + 1) * st]
            i = win.indirect(off[:, fo + k * st:fo + (k + 1) * st])
            addc(eng[k % len(eng)], o, i, bias, r, [w + "_%d" % k], 16 * st * C["G"] + 65)
        return [w + "_%d" % k for k in range(sub)]

    def wrap(out, big, off, src, so, n, r, w, bank):
        mm([(out, big[:, off(i):off(i) + 128], src[:, so + i:so + n:16]) for i in range(16)], r, w, bank)

    offN = lambda i: 15 - i
    NTw = T.NT[:, 0:V]

    def twice(r, s, k, src, key, scale, bias, bank):
        zi = T.Zi[:, k * B:(k + 1) * B]
        act(zi, src, ID, [key], ["zi%d" % k], B, bias=bias, scale=scale, bank=bank)
        e = O["twin"][r][4 * s + k]
        if e == "a":
            act(zat(k), src, ID, [key], ["zw%d" % k], B, bias=bias, scale=scale, bank=bank)
        elif e == "g":
            op("g", lambda: g.affine_select(zat(k), zi, [[0, B]], GE, 0.0, 0, 0), ["zi%d" % k], ["zw%d" % k], 0.17 + 2 * B * cyc)
        else:
            dma("s", zat(k), zi, ["zi%d" % k], ["zw%d" % k], 128 * 2048)

    def step(r, s, h, cvk):
        a, key, o = xi(r, s, h)
        sl = slice(h * HW, (h + 1) * HW)
        ch = (2 * h, 2 * h + 1)
        zo = h * (H + V + S)
        zk = ["zw%d" % k for k in ch]
        how = O["how"][r][h][s - 1]
        st = H // O["sub"][0] if how == "e" else B
        for c in range(0, H, st):
            if how == "e":
                ks = [k for k in ch if c <= (k % 2) * B < c + st]
                vtt(T.cmpb[:, h * H + c:h * H + c + st], Wc.indirect(T.XI[:, o + c // 16:o + (c + st) // 16]),
                    T.Zi[:, h * H + c:h * H + c + st], ALU.is_gt, WK + [key] + ["zi%d" % k for k in ks], ["cmp%d" % k for k in ks],
                    st * C["G"] + 55)
                ops[-1]["due"] = (r, s, ks[0])
            else:
                k = 2 * h + c // B
                wd, zb = slice(k * B, (k + 1) * B), k % 2
                ks = agather(T.Nc, k * B, Wc, T.XI, o + c // 16, 32, WK + [key], "nc%d" % k, bias=0.5 - E)
                mm([(ps[zb][:], T.nI16[:], T.Nc[:, wd])], ["nI16"] + ks, ["b%d" % zb], zb, "open")
                z = (T.I16, T.zbf, "zf%d" % k, 0.0) if s == 1 else (T.Ih, T.Z16, "z%d" % k, E)
                mm([(ps[zb][:], z[0][:], z[1][:, wd])], ["I16", "Ih", z[2]], ["b%d" % zb], zb, "close")
                ops[-1]["due"] = (r, s, k)
                act(T.cmpb[:, wd], ps[zb][:], ACT.Sign, ["b%d" % zb], ["cmp%d" % k], B, bias=z[3] - 0.5, scale=-1.0, bank=zb)
        b = 2 + h
        pq, pt = ps[b][:, 0:HW], ps[b][:, HW:2 * HW]
        lo, jk = (9 * K, "JE") if how == "e" else (K, "JA")
        mm([(pq, T.BigK[:, 15 - i:143 - i], T.cmpb[:, h * H + i:(h + 1) * H:16]) for i in range(16)]
           + [(pq, T.KI[:], T.EQ[:, h * 256 + e * HW:h * 256 + (e + 1) * HW]) for e in range(s - 1)],
           ["cmp%d" % k for k in ch] + ["BigK", "KI"] + ["eq%d_%d" % (h, e) for e in range(s - 1)], ["b%d" % b], b)
        sg = 1.0 if h else -1.0
        xf = T.xf[:, (s % 2) * 128 + h * HW:(s % 2) * 128 + (h + 1) * HW]
        xk = "xf%d_%d" % (s % 2, h)
        act(xf, ps[6 + h][:, PX + (s - 1) * HW:PX + s * HW], ID, ["px%d_%d" % (h, s)], [xk], HW, scale=sg,
            bias=XO - lo - (0 if h else H), bank=6 + h)
        vtt(pt, pq, xf, ALU.max, ["b%d" % b, xk], ["t%d" % b], HW, b)
        vtt(T.tm[:, sl], pt, T[jk][:, sl], ALU.min, ["t%d" % b, jk + str(h)], ["tm%d" % h], HW, b)
        vts(T.I2[:, sl], T.tm[:, sl], lo - XO, sg, ALU.add, ALU.mult, ["tm%d" % h], ["i2%d" % h], HW)
        win = WZ[:, H:2 * H + V + S] if h else WZ[:, 0:H + V]
        st = H // O["sub"][1]
        for c in range(0, H, st):
            ks = [k for k in ch if c <= (k % 2) * B < c + st]
            vtt(T.Z16[:, h * H + c:h * H + c + st], win.indirect(T.I2[:, h * HW + c // 16:h * HW + (c + st) // 16]),
                T.Zi[:, h * H + c:h * H + c + st], ALU.add, WK + zk + ["zi%d" % k for k in ks] + ["i2%d" % h, "dump"],
                ["z%d" % k for k in ks], st * C["G"] + 55)
        for k in ch:
            wd, zb = slice(k * B, (k + 1) * B), k % 2
            if s < 4 and O["f16"]:
                twice(r, s, k, T.Z16[:, wd], "z%d" % k, 0.5, 0.0, None)
            elif s < 4:
                mm([(ps[zb][:], T.Ih[:], T.Z16[:, wd])], ["Ih", "z%d" % k], ["b%d" % zb], zb)
                twice(r, s, k, ps[zb][:], "b%d" % zb, 1.0, 0.0, zb)
            else:
                mm([(ps[zb][:], T.nI16[:], T.cv[:, wd])], ["nI16", cvk[k]], ["b%d" % zb], zb, "open")
                mm([(ps[zb][:], T.Ih[:], T.Z16[:, wd])], ["Ih", "z%d" % k], ["b%d" % zb], zb, "close")
                act(T.zbf[:, wd], ps[zb][:], ACT.Abs, ["b%d" % zb], ["zf%d" % k], B, bias=-E, bank=zb)
                if r == RO - 1:
                    dma("s", T.yz[:, wd], T.zbf[:, wd], ["zf%d" % k], ["yz%d" % k], 128 * 1024)

    def steps(r, ss, cvk):
        for s in ss:
            for h in range(2):
                step(r, s, h, cvk)

    for r in range(RO):
        last = r == RO - 1
        for k in range(4):
            twice(r, 0, k, T.zbf[:, k * B:(k + 1) * B], "zf%d" % k, 1.0, E, None)
        for s in range(1, 5):
            for h in range(2):
                a, key, o = xi(r, s - 1, h)
                ks = agather(T.Nw, h * H, NTw, T.XI, o, HW, NK + [key], "Nw%d" % h, O["csub"], O["chain"][r][2 * (s - 1) + h])
                px = ps[6 + h][:, PX + (s - 1) * HW:PX + s * HW]
                wrap(px, T.BigN, offN, T.Nw, h * H, H, ks + ["BigN"], ["px%d_%d" % (h, s)], 6 + h)
                a, key, o = xi(r, s, h)
                vcp(a, px, ["px%d_%d" % (h, s)], [key], HW, 6 + h)
        n5 = []
        cvk = []
        for h in range(2):
            b = 6 + h
            sl = slice(h * HW, (h + 1) * HW)
            pc, pu, pv = (ps[b][:, PC + k * HW:PC + (k + 1) * HW] for k in range(3))
            wrap(pc, T.BigC, offN, T.zbf, h * H, H, ["zf%d" % (2 * h), "zf%d" % (2 * h + 1), "BigC"], ["pc%d" % h], b)
            vcp(T.ci[:, sl], pc, ["pc%d" % h], ["ci%d" % h], HW, b)
            vts(T.cj[:, sl], T.ci[:, sl], 3, None, ALU.bitwise_and, None, ["ci%d" % h], ["cj%d" % h], HW)
            for s in range(4):
                o = h * 256 + s * HW
                vts(T.EQ[:, o:o + HW], T.cj[:, sl], float(s), None, EQL, None, ["cj%d" % h], ["eq%d_%d" % (h, s)], HW)
            vtt(T.prod[:, h * 256:(h + 1) * 256], ps[b][:, PX:PX + 256], T.EQ[:, h * 256:(h + 1) * 256], ALU.mult,
                ["px%d_%d" % (h, s) for s in range(1, 5)] + ["eq%d_%d" % (h, s) for s in range(4)], ["prod%d" % h], 256, b)
            mm([(pu, T.I32[:], T.prod[:, h * 256 + s * HW:h * 256 + (s + 1) * HW]) for s in range(4)],
               ["I32", "prod%d" % h], ["pu%d" % h], b)
            vcp(T.UI[:, sl], pu, ["pu%d" % h], ["ui%d" % h], HW, b)
            if h == 0:
                act(T.uf[:], ps[b][:, PC + HW:PC + HW + 32], ID, ["pu0"], ["uf"], 32, bank=b)
            ks = agather(T.N5, h * H, NTw, T.UI, h * HW, HW, NK + ["ui%d" % h], "N5%d" % h, 2, "a" if h else O["hops"][1] + "a")
            n5.append(ks)
            wrap(pv, T.BigN, offN, T.N5, h * H, H, ks + ["BigN"], ["pv%d" % h], b)
            a, key, o = xi(r + 1, 0, h)
            vcp(a, pv, ["pv%d" % h], [key], HW, b)
            cvk += agather(T.cv, h * H, Wc, T.XI, o, HW, WK + [key], "cv%d" % h, sub=2, bias=0.5 - E)
        nA = n5[0][0]
        vkey, vo = xi(r + 1, 0, 0)[1:]
        if last:
            dma("g", T.yc[:], T.N5[0:128:16, :], n5[0] + n5[1], ["yc"], 8 * 8192)
            dma("g", T.yc[:], T.N5[1:128:16, :], n5[0] + n5[1] + ["yc"], ["yc"], 8 * 8192, accum_op=ALU.add)
        steps(r, [1], cvk)
        pT, pP, pa, pt, pS, pR, pk = (ps[4][:, a:b] for a, b in ((0, 64), (64, 96), (96, 128), (128, 160), (160, 176),
                                                                 (192, 208), (224, 240)))
        mm([(ps[4][:, 16 * t:16 * t + 16], T.N5[:, 128 * t:128 * (t + 1)], T.SelT[:]) for t in range(4)],
           [nA, "SelT"], ["pT"], 4, "each")
        addc(O["hops"][0], T.hT[:], pT, 0.0, ["pT"], ["hT"], 64, 4)
        mm([(pP, T.Pp[:], T.uf[:])], ["Pp", "uf"], ["pP"], 4)
        act(T.upk[:], pP, ID, ["pP"], ["upk"], 32, bias=2.5 * K, bank=4)
        for gr in range(8):
            lst = []
            kk = []
            for t in range(4):
                o = (gr * 4 + t) * 192
                c = 16 * t + 2 * gr
                vts(T.OH[:, o:o + 64], T.ioA[:], T.hT[:, c:c + 1], None, EQL, None, ["ioA", "hT"], ["oa%d" % o], 32)
                vts(T.OH[:, o + 64:o + 192], T.ioB[:], T.hT[:, c + 1:c + 2], None, EQL, None, ["ioB", "hT"], ["ob%d" % o], 64)
                ops[-1]["spare"] = ops[-2]["spare"] = (7 - gr) * O["spare"]
                kk += ["oa%d" % o, "ob%d" % o]
                lst.append((ps[5][64 * (gr % 2):64 * (gr % 2) + 64, 128 * (gr // 2):128 * (gr // 2) + 128],
                            T.OH[:, o:o + 64], T.OH[:, o + 64:o + 192]))
            mm(lst, kk, ["pH%d" % gr], 5)
            after(["b5"])
        act(T.Hs[:], ps[5][:], ID, ["pH%d" % gr for gr in range(8)] + ["b5"], ["Hs"], 512, bank=5)
        for q in range(4):
            dma("s", T.NT[32 * q + 4:32 * q + 32:16, 0:V], T.Hs[:, 128 * q:128 * (q + 1)], ["Hs"], ["NTc%d" % q], 128 * 256)
        agather(T.aw, 0, NTw, T.XI, vo, 32, NK + [vkey], "aw")
        wrap(pa, T.BigP, lambda i: 16 - (i & ~1), T.aw, 0, A, ["aw_0", "BigP"], ["pa"], 4)
        vtt(pt, pa, T.upk[:], ALU.max, ["pa", "upk"], ["pt"], 32, 4)
        if not last:
            vts(T.nb[:], pa, 2.5 * K, 0.5, ALU.is_gt, ALU.mult, ["pa"], ["nb"], 32, 4)
        vtt(T.tc[:], pt, T.Dc[:], ALU.min, ["pt", "Dc"], ["tc"], 32, 4)
        vts(T.CI[:], T.tc[:], -2.5 * K, None, ALU.add, None, ["tc"], ["CI"], 32)
        if last:
            dma("g", T.Y[0:128:16, 0:V], T.NT[0:128:16, 0:V], ["NTh"], ["Y"], 8 * 32768)
            dma("g", T.Y[0:128:16, 0:V], T.NT[1:128:16, 0:V], ["NTl", "Y"], ["Y"], 8 * 32768 * 2, accum_op=ALU.add,
                max_dma_last_dim=4096)
            mm([(ps[5][:], T.BigN[:, 15:143], T.N5[:, 0:A])], ["BigN", nA], ["b5"], 5)
            act(T.v32[:], ps[5][:], ID, ["b5"], ["v32"], A, bank=5)
            vcp(T.Y[:].indirect(T.CI[:]), T.v32[:], ["CI", "v32", "Y"], ["Y"], A * C["SC"] + 55)
            dma("s", T.yn[:], T.Y[0:128:16, 0:V], ["Y"], ["yn"], 8 * 32768)
        else:
            vcp(T.NT[:].indirect(T.CI[:]), T.N5[:, 0:A], ["CI", nA], NK, A * C["SC"] + 55)
        if not last:
            snd = T["snd%d" % r]
            land = T["land%d" % r]
            mm([(pS, T.Blk[:], T.nb[:, e:32:2]) for e in range(2)], ["Blk", "nb"], ["pS"], 4)
            op("v", lambda pS=pS: g.vector.tensor_tensor_scan(T.Sc[:, 0:16], T.one32[:, 0:16], pS, 0.0, ALU.mult, ALU.add),
               ["pS", "one32"], ["Sc"], dv(32), 4)
            vtt(T.ae[:], T.nb[:], T.Ec[:], ALU.mult, ["nb", "Ec"], ["ae"], 64)
            mm([(pR, T["U%d" % e][:], T.nb[:, e:32:2]) for e in range(2)] + [(pR, T["S%d" % e][:], T.ae[:, e:32:2]) for e in range(2)]
               + [(pR, T.I32[:], T.J[:, 0:16]), (pR, T.nI32[:], T.Sc[:, 0:16])],
               ["U0", "U1", "S0", "S1", "nb", "I32", "J", "ae", "nI32", "Sc"], ["pR"], 4)
            vcp(T.PI[:], pR, ["pR"], ["PI"], 16, 4)
            mm([(ps[5][:, 0:S], T.I16[:], T.N5[:, 0:A:2]), (ps[5][:, 0:S], T.Sh2[:], T.N5[:, 1:A:2])],
               ["I16", "Sh2", nA], ["b5"], 5)
            act(T.pk2[:], ps[5][:, 0:S], ID, ["b5"], ["pk2"], S, bank=5)
            vcp(T.CV[:].indirect(T.PI[:]), T.pk2[:], ["PI", "pk2"], ["CV"], S * C["SC"] + 55)
            mm([(pk, T["BigM" if i % 2 else "BigN"][:, 15 - i:143 - i], T.CV[:, i // 2:128:8]) for i in range(16)],
               ["CV", "BigN", "BigM"], ["pk"], 4)
            vcp(T.TI[:], pk, ["pk"], ["TI"], 16, 4)
            agather(snd, 0, Wc, T.TI, 0, 16, WK + ["TI"], "snd%d" % r, 1, O["hops"][2], 0.5 - E)
            act(snd[:, S:S + 1], T.Sc[:, 15:16], ID, ["Sc"], ["sndc%d" % r], 1, bias=float(A), scale=-2.0)

            def send(snd=snd, land=land, r=r):
                tr = []
                for d in range(N - 1):
                    dst = T.cores[(rank + 1 + d) % N]
                    rid, pid, se = topo.addr(dst)
                    en = topo.engines(core, dst)[4 * d:4 * d + 4]
                    tr.append(RemoteDMATransfer(dst_ids=[DstId(rid=rid, pnc=pid)], dma_engine_mask=sum(1 << e for e in en),
                                                remote_sem=T.sem["arr%d" % r], src=snd[:], dst=land[:, d * SW:(d + 1) * SW]))
                g.remote_dma_fused(tr, local_sem=T.sem.sent)
                return None
            op("g", send, ["snd%d_0" % r, "sndc%d" % r], ["land%d" % r], 1.0, None, "rem", ("arr%d" % r, 12), 128 * 528 * 6)
        steps(r, [2, 3, 4], cvk)
        if not last:
            pd = ps[5][:, 0:SW]
            mm([(pd, T.Psh[:, ((d - r) % 3) * 128:((d - r) % 3) * 128 + 128], land[:, d * SW:(d + 1) * SW]) for d in range(3)],
               ["Psh", "land%d" % r], ["b5"], 5)
            addc(O["hops"][3], T.arr[:], ps[5][:, 0:S], E - 0.5, ["b5"], ["arr"], S, 5)
            vtt(T.nmin[:, 0:1], ps[5][:, S:S + 1], snd[:, S:S + 1], ALU.min, ["b5", "sndc%d" % r], ["nmin"], 1, 5)
            vts(T.q1[:], T.J[:, 0:16], T.nmin[:, 0:1], K, GE, ALU.mult, ["J", "nmin"], ["q1"], 16)
            vtt(T.q2[:], pk, T.q1[:], ALU.max, ["pk", "q1"], ["q2"], 16, 4)
            vtt(T.q3[:], T.q2[:], T.Dk[:], ALU.min, ["q2", "Dk"], ["q3"], 32)
            vcp(T.DI[:], T.q3[:], ["q3"], ["DI"], 16)
            vcp(WZ[:, H:H + V + S].indirect(T.DI[:]), T.arr[:], ["DI", "arr"], WK + ["dump"], S * C["SC"] + 55)
    return ops


def depend(ops):
    lastw, readers, prevq = {}, {}, {}
    for i, o in enumerate(ops):
        d = set()
        for k in o["r"]:
            if k in lastw:
                d.add(lastw[k])
        for k in o["w"] + o.get("after", []):
            if k in lastw:
                d.add(lastw[k])
            d.update(readers.get(k, []))
        d.discard(i)
        o["dep"] = sorted(d)
        o["prev"] = None
        if o["eng"] == "s" and o["w"][0][:2] in ("nx", "zf", "CT", "NT") and o["w"][0][:3] != "NTc":
            o["prev"] = prevq.get("s")
            prevq["s"] = i
        for k in o["r"]:
            readers.setdefault(k, []).append(i)
        for k in o["w"]:
            lastw[k] = i
            readers[k] = []
    return ops


def listsched(P, pr, eager):
    eng, bank, dur, isd, tb, succ, left0, sy, d0 = P
    n = len(eng)
    left = list(left0)
    free, ready, cand = [0.0] * 5, [[] for _ in range(5)], [None] * 5
    held = [[0.0] * 3 for _ in range(8)]
    rt, start = [0.0] * n, [0.0] * n
    pipe, end, seq = 0.0, 0.0, []
    for i in range(n):
        if left[i] == 0:
            ready[eng[i]].append(i)
    for _ in range(n):
        best = None
        for e in range(5):
            if cand[e] is None:
                if not ready[e]:
                    continue
                f, top = free[e], -1e9
                for i in ready[e]:
                    t, b = rt[i], bank[i]
                    if b is not None and held[b][e] > t:
                        t = held[b][e]
                    if t < f:
                        t = f
                    if pr[i] - eager * t > top:
                        top, cand[e] = pr[i] - eager * t, (t, i)
            if best is None or cand[e][0] < best[0]:
                best = cand[e]
        t, i = best
        e, b = eng[i], bank[i]
        ready[e].remove(i)
        seq.append(i)
        start[i] = t
        free[e] = f = t + dur[i]
        cand[e] = None
        if b is not None:
            for x in (0, 1, 2):
                if x != e:
                    held[b][x] = f + sy
                    if cand[x] is not None and bank[cand[x][1]] == b:
                        cand[x] = None
        if isd[i]:
            pipe = max(pipe, f + d0 * 0.7) + tb[i]
            f = pipe + d0 * 0.3
        end = max(end, f)
        for j, real in succ[i]:
            if real and f + sy > rt[j]:
                rt[j] = f + sy
            left[j] -= 1
            if left[j] == 0:
                ready[eng[j]].append(j)
                cand[eng[j]] = None
    return seq, start, end


def replay(P, dep, seq):
    eng, bank, dur, isd, tb, succ, left0, sy, d0 = P
    free = [0.0] * 5
    held = [[0.0] * 3 for _ in range(8)]
    fin = [0.0] * len(eng)
    pipe = 0.0
    for i in seq:
        e, b = eng[i], bank[i]
        t = free[e]
        for j in dep[i]:
            if fin[j] > t:
                t = fin[j]
        if b is not None:
            t = max(t, held[b][e]) + dur[i]
            for x in (0, 1, 2):
                if x != e:
                    held[b][x] = t + sy
        else:
            t += dur[i]
        free[e] = t
        if isd[i]:
            pipe = max(pipe, t + d0 * 0.7) + tb[i]
            t = pipe + d0 * 0.3
        fin[i] = t + sy
    return max(fin)


def plan(mk, C, O, vary):
    ops = mk(C)
    n = len(ops)
    succ, left = [[] for _ in range(n)], [0] * n
    for i, o in enumerate(ops):
        for j in sorted(set(o["dep"] + ([o["prev"]] if o["prev"] is not None else []))):
            succ[j].append((i, j in o["dep"]))
            left[i] += 1

    def table(ops, C):
        return (["vapgs".index(o["eng"]) for o in ops], [o["bank"] for o in ops], [o["dur"] for o in ops],
                [o["kind"] != "c" for o in ops], [o["nb"] / C["rate"] for o in ops], succ, left, C["sync"], C["dma0"])
    P = table(ops, C)
    alt = [table(mk(dict(C, **m)), dict(C, **m)) for m in vary]
    dep = [o["dep"] for o in ops]
    pr = np.zeros(n)
    t0, pace, gap, end = O["pace"]
    for i in range(n - 1, -1, -1):
        o = ops[i]
        late = min([-pr[j] - (C["sync"] if ops[j]["eng"] in ("p", o["eng"]) else O["hop"]) for j, _ in succ[i]] + [end]) - o["dur"] - o.get("spare", 0.0) \
            - (0.0 if o["kind"] == "c" else C["dma0"] + o["nb"] / C["rate"])
        if "due" in o:
            r, s, k = o["due"]
            late = min(late, t0 + (4 * pace + gap) * r + pace * (s - 1 + (k // 2) * O["skew"] + (k % 2) / 4))
        pr[i] = -late

    rs = np.random.RandomState(O["seed"])
    seq, st, end = listsched(P, pr.tolist(), O["eager"])
    a0 = np.array([end] + [replay(x, dep, seq) for x in alt])
    w = np.array([2.0] + [1.0] * len(alt)) / a0
    w = w / np.dot(a0, w) * a0[0]
    cur = best = float(np.dot(a0, w))
    st, out, cur0 = np.array(st), (seq, a0), end
    for it in range(O["iters"]):
        p = pr.copy()
        k = rs.randint(4)
        if k == 0:
            a = rs.randint(n)
            p[a:a + rs.randint(1, 40)] += rs.normal(0, 3.0)
        elif k == 2:
            p[rs.randint(n, size=3)] += rs.normal(0, 2.0, 3)
        else:
            t = rs.rand() * st.max()
            m = (abs(st - t) < 3) & (rs.rand(n) < 0.3) if k == 1 else abs(st - t) < 6
            p[m] += rs.normal(0, 1.5 if k == 1 else 0.4, m.sum())
        seq, start, end = listsched(P, p.tolist(), O["eager"])
        slack = O["temp"] * (1 - it / O["iters"]) * rs.exponential()
        if end > cur0 + 1.5 + slack:
            continue
        a = np.array([end] + [replay(x, dep, seq) for x in alt])
        s = float(np.dot(a, w))
        if s <= cur + slack:
            cur, cur0, pr, st = s, end, p, np.array(start)
            if s < best:
                best, out = s, (seq, a)
    return out


def polish(mk, C, O, vary, seq):
    ops = mk(C)
    n = len(ops)
    eng = ["vapgs".index(o["eng"]) for o in ops]
    bank = [o["bank"] for o in ops]
    dep = [o["dep"] for o in ops]
    pre = [set(o["dep"] + ([o["prev"]] if o["prev"] is not None else [])) for o in ops]
    isd = [o["kind"] != "c" for o in ops]
    var = []
    for m in [{}] + vary:
        C2 = dict(C, **m)
        o2 = mk(C2)
        var.append(([o["dur"] for o in o2], [o["nb"] / C2["rate"] for o in o2], C2["sync"], C2["dma0"]))

    def run(seq, v):
        dur, tb, sy, d0 = v
        free, who = [0.0] * 5, [-1] * 5
        held = [[0.0, 0.0, 0.0, -1, -1, -1] for _ in range(8)]
        fin, why, res = [0.0] * n, [-1] * n, [True] * n
        pipe = 0.0
        for i in seq:
            e = eng[i]
            t, y, q = free[e], who[e], True
            for j in dep[i]:
                if fin[j] > t:
                    t, y, q = fin[j], j, False
            b = bank[i]
            if b is not None:
                hb = held[b]
                if hb[e] > t:
                    t, y, q = hb[e], hb[3 + e], True
                t += dur[i]
                for x in (0, 1, 2):
                    if x != e:
                        hb[x], hb[3 + x] = t + sy, i
            else:
                t += dur[i]
            free[e], who[e], why[i], res[i] = t, i, y, q
            if isd[i]:
                pipe = max(pipe, t + d0 * 0.7) + tb[i]
                t = pipe + d0 * 0.3
            fin[i] = t + sy
        end = max(fin)
        i, arcs = fin.index(end), []
        while i >= 0:
            if res[i] and why[i] >= 0 and why[i] not in pre[i]:
                arcs.append((why[i], i))
            i = why[i]
        return end, arcs

    def swap(seq, j, i):
        a, b = seq.index(j), seq.index(i)
        need, wait, engs, banks = [i], set(pre[i]), set(), set()
        for x in seq[b - 1:a:-1]:
            if x in wait or eng[x] in engs or (bank[x], eng[x]) in banks or eng[x] == eng[i] \
                    or (bank[x] is not None and bank[x] == bank[i]):
                need.append(x)
                wait |= pre[x]
                engs.add(eng[x])
                if bank[x] is not None:
                    banks.update((bank[x], e) for e in range(3) if e != eng[x])
        if j in wait or eng[j] in engs or (bank[j], eng[j]) in banks:
            return None
        s = set(need)
        return seq[:a] + need[::-1] + [x for x in seq[a:b] if x not in s] + seq[b + 1:]

    res = [run(seq, v) for v in var]
    w = np.array([2.0] + [1.0] * len(vary)) / np.array([r[0] for r in res])
    w = (w / np.dot(w, [r[0] for r in res]) * res[0][0]).tolist()
    total = lambda res: sum(a * r[0] for a, r in zip(w, res))
    cur = best = total(res)
    out = (list(seq), np.array([r[0] for r in res]))
    rs = np.random.RandomState(O["seed"])
    for it in range(O["moves"]):
        arcs = res[rs.randint(len(res))][1]
        if not arcs:
            continue
        j, i = arcs[rs.randint(len(arcs))]
        s2 = swap(seq, j, i)
        for _ in range(rs.geometric(O["far"]) - 1):
            if s2 is None:
                break
            p = s2.index(i) - 1
            while p >= 0 and eng[s2[p]] != eng[i]:
                p -= 1
            s3 = swap(s2, s2[p], i) if p >= 0 and s2[p] not in pre[i] else None
            if s3 is None:
                break
            s2 = s3
        if s2 is None:
            continue
        slack = O["heat"] * (1 - it / O["moves"]) * rs.exponential()
        r0 = run(s2, var[0])
        if r0[0] > res[0][0] + 1.0 + 2 * slack:
            continue
        r2 = [r0] + [run(s2, v) for v in var[1:]]
        s = total(r2)
        if s <= cur + slack:
            cur, seq, res = s, s2, r2
            if s < best:
                best, out = s, (list(seq), np.array([r[0] for r in res]))
    return out


def rank_program(g, core, T, topo):
    if T.rank_of(core) is None:
        return
    mk = lambda C: depend(build(g, core, T, topo, C, OPT))
    if "seq" not in PLAN:
        PLAN["seq"], PLAN["est"] = polish(mk, COST, OPT, VARY, plan(mk, COST, OPT, VARY)[0])
    ops = mk(COST)
    seq = PLAN["seq"]
    queue = {"v": g.vector, "a": g.scalar, "p": g.tensor, "g": g, "s": g.sync}
    final, cnt, nd = {}, {e: 0 for e in "vapg"}, 0
    last = {b: {} for b in range(8)}
    for at, i in enumerate(seq):
        o = ops[i]
        o["at"] = at
        if o["bank"] is not None:
            o["dep"] = o["dep"] + [j for e, j in last[o["bank"]].items() if e != o["eng"]]
            last[o["bank"]][o["eng"]] = i
        if o["kind"] == "c":
            cnt[o["eng"]] += 1
            o["sig"] = ("s" + o["eng"], cnt[o["eng"]])
        elif o["kind"] == "dma":
            o["sig"] = ("d%d" % nd, 16)
            nd += 1
        else:
            o["sig"] = o["ext"]
            final["sent"] = final.get("sent", 0) + 12
        final[o["sig"][0]] = o["sig"][1]
    seen = {e: {} for e in queue}
    for i in seq:
        o = ops[i]
        know = seen[o["eng"]]
        for j in sorted(o["dep"], key=lambda j: -ops[j]["at"]):
            s, v = ops[j]["sig"]
            if v > know.get(s, 0):
                queue[o["eng"]].wait_ge(T.sem[s], v)
                know[s] = v
                for s2, v2 in ops[j]["knew"].items():
                    know[s2] = max(know.get(s2, 0), v2)
        o["knew"] = dict(know) if o["kind"] != "rem" else {}
        ins = o["fn"]()
        if o["kind"] != "rem":
            ins.then_inc(T.sem[o["sig"][0]], 1 if o["kind"] == "c" else 16)
    for s in sorted(final):
        if final[s] > seen["g"].get(s, 0):
            g.wait_ge(T.sem[s], final[s])
